import numpy as np, ml_dtypes
CORES = [2,3,42,43,82,83,122,123]
N = 8
import mx_ref
BF = ml_dtypes.bfloat16
def entries(a):
    return np.ascontiguousarray(a.T).reshape(-1)
def table(e):
    return np.ascontiguousarray(np.reshape(e, (-1, 16)).T).astype(np.int32)
def pick(q, e):
    c = np.concatenate([q[0].reshape(128, -1, 4), np.zeros((128, 1, 4), np.uint8)], axis=1); s = np.concatenate([q[1], np.ones((16, 1), np.uint8)], axis=1)
    return (np.ascontiguousarray(c[:, e].reshape(128, -1)), np.ascontiguousarray(s[:, e]))
def join(*qs):
    return (np.concatenate([q[0] for q in qs], axis=1), np.concatenate([q[1] for q in qs], axis=1))
def put(q, e, v):
    c, s = q[0].reshape(128, -1, 4).copy(), q[1].copy(); c[:, e] = v[0].reshape(128, -1, 4); s[:, e] = v[1]
    return (c.reshape(128, -1), s)
def pk(c, s):
    return (np.ascontiguousarray(c), mx_ref.live(s))
def emit(q):
    return q[0], q[1]
def decode(q):
    o = []
    for b in range(4):
        e = np.zeros((128, 128, 4), np.float32); e[np.arange(128), np.arange(128), b] = 1
        o.append(mx_ref.matmul(mx_ref.quantize(e.reshape(128, 512).astype(BF)), q))
    return np.stack(o, axis=2).reshape(128, -1)
def cut(t, i, w=512):
    return t[:, w * i:w * i + w]
def f(rng, *shape):
    return mx_ref.flush((rng.standard_normal(shape, dtype=np.float32) * np.exp2(rng.integers(-2, 3, shape[:-1] + (1,)))).astype(BF))
def wide(rng, *shape, cols=0):
    v = rng.standard_normal(shape, dtype=np.float32) * np.exp2(rng.integers(-12, 13, shape)).astype(np.float32)
    if cols: v *= np.repeat(np.exp2(rng.integers(-cols, cols + 1, shape[:-2] + (1, shape[-1] // 4))) * (rng.random(shape[:-2] + (1, shape[-1] // 4)) > 0.0625), 4, axis=-1).astype(np.float32)
    return mx_ref.flush(v.astype(BF))
V, E, PAIR, CAP, R, O = 48, 192, 24, 8, 2, 2
def lift(v):
    v = np.array(v, np.float32)
    v[np.abs(v) < np.float32(2.0 ** -12)] = 0
    return v.astype(BF)
def lay(back):
    return np.stack([table(back[E * r:E * r + E]) for r in range(N)])
def links(rng):
    back = np.zeros(N * E, int)
    part = [rng.permutation(E).reshape(N, PAIR) + E * r for r in range(N)]
    for r in range(N):
        for h in range(r, N):
            a, c = part[r][h], part[h][r]
            if h == r: a, c = a[:PAIR // 2], a[PAIR // 2:]
            back[a] = c
            back[c] = a
    return lay(back)
def setup_inputs(rng):
    return {"b": lift(f(rng, N, 128, 4 * V)), "m": lift(f(rng, N, 128, 4 * E)), "u": f(rng, N, 128, 512), "w": f(rng, N, 128, 512 * O), "rev": links(rng)}
def setup_inputs_ties(rng):
    d = setup_inputs(rng)
    x = rng.integers(4, 8, (128, 1, 4)) * np.exp2(rng.integers(-2, 1, (128, 1, 4))) * rng.choice([-1.0, 1.0], (128, 1, 4))
    double = rng.permutation(N) < N // 2
    d["b"] = np.stack([np.repeat(x * (1 + double[r]), V, axis=1).reshape(128, 4 * V) for r in range(N)]).astype(np.float32).astype(BF)
    d["m"] = np.stack([np.repeat(x, E, axis=1).reshape(128, 4 * E) for r in range(N)]).astype(np.float32).astype(BF)
    return d
def setup_inputs_near(rng):
    d = setup_inputs(rng)
    p = 8 * rng.permutation(16)[:3] + rng.integers(0, 8, 3)
    t = rng.integers(0, 4, 3)
    i = np.arange(V)
    rows = [np.full(V, 32), 4 * (i % 8), 4 * (i // 8)]
    g = 1.0 - 2 * rng.integers(0, 2, N)
    b, m, u = np.array(d["b"]).reshape(N, 128, V, 4), np.array(d["m"]).reshape(N, 128, E, 4), np.array(d["u"])
    u[:, :, :4] = 0
    for k in range(3):
        b[:, p[k], :, t[k]] = np.broadcast_to(rows[k], (N, V)).astype(np.float32).astype(BF)
        m[:, p[k], :, t[k]] = 0
        u[:, p[k], t[k]] = (g * 2.0 ** (0, -19, -16)[k]).astype(np.float32).astype(BF)
    d["b"], d["m"], d["u"] = b.reshape(N, 128, 4 * V), m.reshape(N, 128, 4 * E), u
    return d
def setup_inputs_huge_order(rng):
    d = setup_inputs(rng)
    for k, n in (("b", V), ("m", E)):
        sign = np.repeat(1 - 2 * rng.integers(0, 2, (N, 1, n)), 4, axis=2)
        d[k] = ((1 + rng.random((N, 128, 4 * n))) * 2.0 ** 27 * sign).astype(np.float32).astype(BF)
    u = np.array(d["u"])
    u[:, :, :4] = ((1 + rng.random((N, 128, 4))) * 2.0 ** 29 * (1 - 2 * rng.integers(0, 2, (N, 1, 1)))).astype(np.float32).astype(BF)
    d["u"] = u
    for g in rng.permutation(16)[:2]:
        x = rng.integers(4, 8, (8, 1, 4)) * 2.0 ** 25 * rng.choice([-1.0, 1.0], (8, 1, 4))
        kind = rng.integers(-1, 2, (N, 1, E, 1))
        small = rng.integers(1, 8, (N, 8, E, 4)) * 0.25 * rng.choice([-1.0, 1.0], (N, 8, E, 4))
        nodes = x * (1 - 2 * rng.integers(0, 2, (N, 1, V, 1)))
        d["b"][:, 8 * g:8 * g + 8] = nodes.reshape(N, 8, 4 * V).astype(np.float32).astype(BF)
        d["m"][:, 8 * g:8 * g + 8] = np.where(kind == 0, small, x * kind).reshape(N, 8, 4 * E).astype(np.float32).astype(BF)
    return d
def setup_inputs_blocks(rng):
    d = setup_inputs(rng)
    spots = [np.arange(V).reshape(N, PAIR // 4)[rng.permutation(N)] + V * r for r in range(N)]
    back, keep, four = np.zeros(N * E, int), np.zeros(N * V, bool), np.arange(4)
    for r in range(N):
        for h in range(r, N):
            a, c = spots[r][h], rng.permutation(spots[h][r])
            if h == r: c = a
            for k in range(PAIR // 4):
                q = rng.permutation(4)
                if h == r:
                    back[4 * a[k] + q] = 4 * a[k] + q[[1, 0, 3, 2]]
                else:
                    back[4 * a[k] + four] = 4 * c[k] + q
                    back[4 * c[k] + q] = 4 * a[k] + four
            on = rng.integers(0, PAIR // 4)
            if (r + h) % 2 == 0:
                keep[a[on]] = True
                keep[c[on]] = True
            else:
                keep[a] = True
                keep[c] = True
    d["b"] = np.where(np.repeat(keep.reshape(N, 1, V), 4, axis=2), d["b"], np.zeros_like(d["b"]))
    d["m"] = np.where(np.repeat(keep.reshape(N, 1, V), 16, axis=2), d["m"], np.zeros_like(d["m"]))
    d["rev"] = lay(back)
    return d
def setup_inputs_spread(rng):
    d = {**setup_inputs(rng), "b": lift(wide(rng, N, 128, 4 * V, cols=6)), "m": lift(wide(rng, N, 128, 4 * E, cols=6))}
    u = np.array(d["u"])
    u[int(rng.integers(0, N)), :, :4] = 0
    return {**d, "u": u}
def check_inputs(d):
    bad = []
    for k, low, high in (("b", -12, 28), ("m", -12, 28), ("u", -30, 30), ("w", -30, 30)):
        v = np.abs(d[k].astype(np.float32))
        if not (np.isfinite(v).all() and ((v == 0) | (v >= 2.0 ** low) & (v <= 2.0 ** high)).all()): bad.append("a value of " + k)
    back = np.concatenate([entries(d["rev"][r]) for r in range(N)])
    if back.min() < 0 or back.max() >= N * E:
        bad.append("rev is out of range")
        return bad
    e = np.arange(N * E)
    if (back[back] != e).any() or (back == e).any(): bad.append("rev isn't made of pairs of different edges")
    if (np.bincount(e // E * N + back // E, minlength=N * N) != PAIR).any(): bad.append("edges of a pair of ranks")
    return bad
def reference(b, m, u, w, rev):
    y, up = np.zeros((N, 128, R * O * E), np.float32), np.zeros((N, 1, E), np.float32)
    oc, osc = np.zeros((N, 128, 4 * E), np.uint8), np.zeros((N, 16, E), np.uint8)
    back = np.concatenate([entries(rev[r]) for r in range(N)])
    e = np.arange(N * E)
    head = back // E
    others = np.array([[k for k in range(4) if k != j] for j in range(4)])
    come = back[4 * (e // 4)[:, None] + others[e % 4]]
    msg = mx_ref.quantize(np.concatenate([m[r] for r in range(N)], axis=1))
    dm = decode(msg).reshape(128, N * E, 4)
    db = decode(mx_ref.quantize(np.concatenate([b[r] for r in range(N)], axis=1))).reshape(128, N * V, 4)
    qu = [mx_ref.quantize(np.ascontiguousarray(u[r])) for r in range(N)]
    qw = [[mx_ref.quantize(np.ascontiguousarray(cut(w[r], o))) for o in range(O)] for r in range(N)]
    for t in range(R):
        z = db[:, e // 4]
        for j in range(3): z = z + dm[:, come[:, j]]
        z = z * np.float32(0.25)
        cand = mx_ref.quantize(np.ascontiguousarray(z.reshape(128, -1).astype(BF)))
        dc = decode(cand).reshape(128, N * E, 4)
        change = mx_ref.quantize(np.ascontiguousarray((dc - dm).reshape(128, -1).astype(BF)))
        taken = []
        for r in range(N):
            s = np.abs(mx_ref.matmul(qu[r], pick(change, np.arange(E * r, E * r + E)))[0]) + np.float32(0)
            for h in range(N):
                k = np.flatnonzero(head[E * r:E * r + E] == h)
                k = k[np.argsort(-s[k], kind="stable")[:CAP]]
                up[r, 0, k] += 1
                taken.append(E * r + k)
        taken = np.concatenate(taken)
        msg = put(msg, taken, pick(cand, taken))
        dm[:, taken] = dc[:, taken]
        for r in range(N):
            new = np.arange(E * r, E * r + E) if t == 0 else taken[N * CAP * r:N * CAP * r + N * CAP]
            now = pick(msg, new)
            for o in range(O):
                i = (t * O + o) * E
                if t > 0: y[r, :, i:i + E] = y[r, :, i - O * E:i - O * E + E]
                y[r][:, i + new - E * r] = mx_ref.matmul(qw[r][o], now)
    for r in range(N): oc[r], osc[r] = emit(pick(msg, np.arange(E * r, E * r + E)))
    return {"y": y, "oc": oc, "osc": osc, "up": up}

@@ -1,0 +1,442 @@
+from concourse.bass import DstId, RemoteDMATransfer
+from concourse.mybir import dt, AluOpType, AxisListType, ActivationFunctionType
+
+E = 192
+PAIR = 24
+CAP = 8
+FAR = 256
+X4 = "float8_e4m3fn_x4"
+
+
+def _sb(n, d):
+    return ("sbuf", [128, n], d)
+
+
+SCRATCH = {"ps": ("psum", [128, 4096], "float32")}
+for _n, _w in (("q0", E), ("mc0", FAR + E), ("mc1", FAR + E), ("land0", 240), ("land1", 240), ("a0", 3 * E), ("a1", 3 * E),
+               ("qb", 128), ("bx", E), ("qu", 128), ("ur", 128), ("qw", 256), ("ep", 512), ("en", 512), ("yq", E),
+               ("xq", 128), ("wq", 128), ("m1e", E), ("m2s", E), ("m2e", E)):
+    SCRATCH[_n + "c"] = _sb(_w, X4)
+    SCRATCH[_n + "s"] = _sb(_w, "uint8")
+for _n, _w in (("mt", 4 * E), ("bt", 512), ("ut", 512), ("wt", 1024), ("zt", 4 * E), ("yt", 4 * E), ("xt", 512), ("wsel", 512),
+               ("etp", 528), ("etn", 528), ("ones", 128), ("ident", 128), ("hb", 16), ("junk", 10 * E), ("cmp", 2 * 208),
+               ("hi2", 16), ("src0", E), ("src", E), ("swin", 2 * E), ("swt", 2 * E), ("l32", 16), ("p32", 16), ("lb", E),
+               ("lrow", E), ("pb", E), ("prow", E), ("pd", E), ("pdt", E), ("ag", 3 * E), ("agt", 3 * E), ("qi", 16),
+               ("beats", 96), ("rst", 96), ("cnt", 96), ("win0", FAR + E), ("win1", FAR + E), ("ups", E)):
+    SCRATCH[_n] = _sb(_w, "bfloat16")
+for _n, _w in (("pc", 8), ("c2", 12), ("econ", E), ("kb", E), ("krow", E), ("revf", 16), ("revb", E), ("rrow", E), ("xk", 8),
+               ("xr", 8), ("q2", 8), ("sm", 64), ("n48", 48), ("c16", 12), ("base", 12), ("cc", 12), ("k8", 12), ("i16", 128),
+               ("blf", 12), ("thr", 96), ("t2", 96), ("t1", 96), ("arow", E), ("ncol", 8), ("dd", 96), ("offf", 16),
+               ("y0", 2 * E), ("y1", 2 * E), ("upe", E), ("lt", 32), ("ff", 64)):
+    SCRATCH[_n] = _sb(_w, "float32")
+for _n, _w in (("wr", 16), ("pint", 8), ("pi2", 8), ("sw", 16), ("sd", 16), ("fi", 64)):
+    SCRATCH[_n] = _sb(_w, "int32")
+for _n, _w in (("qoff", 12), ("soff", 12), ("list16", 2), ("foff", 36), ("aoff", 36), ("boff", 12), ("bl", 12),
+               ("dupl", 12), ("poff", 12), ("zoff", 8), ("cl", 8), ("off0", 12), ("off1", 12)):
+    SCRATCH[_n] = _sb(_w, "uint16")
+
+SEMAPHORES = ["cv", "ca", "cp", "cg", "ldr", "ldm", "ldb", "ldu", "ldw", "sent", "arrc0", "arrs0", "arrc1", "arrs1",
+              "sty", "sto"]
+
+Op = AluOpType
+Act = ActivationFunctionType
+
+
+def _masks(T, topo, r):
+    n = len(T.cores)
+    me = T.cores[r]
+    order = [(r + k) % n for k in range(1, n)]
+    far = [h for h in order if topo.chip(T.cores[h]) != topo.chip(me)]
+    near = [h for h in order if topo.chip(T.cores[h]) == topo.chip(me)]
+    eng = topo.engines(me, T.cores[far[0]])
+    ev, od = eng[0::2], eng[1::2]
+    codes = [[ev[0]], [ev[1]], [ev[2]], [ev[3]], od[0:2], od[2:4]]
+    scales = [ev[0:2], ev[2:4], [od[0]], [od[1]], [od[2]], [od[3]]]
+    out = {}
+    for k, h in enumerate(far):
+        out[h] = (codes[k], scales[k])
+    for h in near:
+        rest = [e for e in topo.engines(me, T.cores[h]) if e not in eng]
+        out[h] = ([rest[0]], [rest[2]])
+    return out
+
+
+def rank_program(g, core, T, topo):
+    r = T.rank_of(core)
+    if r is None:
+        return
+    n_ranks = len(T.cores)
+    eng = {"v": g.vector, "a": g.scalar, "p": g.tensor, "g": g, "s": g.sync}
+    own = {"v": "cv", "a": "ca", "p": "cp", "g": "cg"}
+    count = {"cv": 0, "ca": 0, "cp": 0, "cg": 0}
+    waited = {q: {} for q in eng}
+    lastw, readers = {}, {}
+
+    def need(q, reads, writes):
+        deps = {}
+        for k in list(reads) + list(writes):
+            if k in lastw:
+                s, v = lastw[k]
+                deps[s] = max(deps.get(s, 0), v)
+        for k in writes:
+            for s, v in readers.get(k, []):
+                deps[s] = max(deps.get(s, 0), v)
+        for s, v in deps.items():
+            if q == "p" and s == "cp":
+                continue
+            if waited[q].get(s, 0) < v:
+                eng[q].wait_ge(T.sem[s], v)
+                waited[q][s] = v
+
+    def mark(tok, reads, writes):
+        for k in reads:
+            readers.setdefault(k, []).append(tok)
+        for k in writes:
+            lastw[k] = tok
+            readers[k] = []
+
+    def op(q, call, reads, writes):
+        need(q, reads, writes)
+        s = own[q]
+        count[s] += 1
+        call().then_inc(T.sem[s], 1)
+        mark((s, count[s]), reads, writes)
+
+    def dma(q, out, in_, sem, reads, writes):
+        need(q, reads, writes)
+        count[sem] = count.get(sem, 0) + 16
+        eng[q].dma_start(out, in_).then_inc(T.sem[sem], 16)
+        mark((sem, count[sem]), reads, writes)
+
+    V, A = g.vector, g.scalar
+
+    def ts(out, in0, s1, s2, o0, o1, reads, writes):
+        if o1 is None:
+            op("v", lambda: V.tensor_scalar(out, in0, s1, None, o0), reads, writes)
+        else:
+            op("v", lambda: V.tensor_scalar(out, in0, s1, s2, o0, o1), reads, writes)
+
+    def tt(out, in0, in1, o, reads, writes):
+        op("v", lambda: V.tensor_tensor(out, in0, in1, o), reads, writes)
+
+    def cp(out, in_, reads, writes):
+        op("v", lambda: V.tensor_copy(out, in_), reads, writes)
+
+    def act(out, in_, func, reads, writes, **kw):
+        op("a", lambda: A.activation(out, in_, func, **kw), reads, writes)
+
+    def fill(ap, c, writes):
+        op("v", lambda: V.memset(ap, c), [], writes)
+
+    def tr(out, in_, reads, writes):
+        op("v", lambda: V.transpose(out, in_), reads, writes)
+
+    def iota(out, pat, base, cm, writes, small=True):
+        if small:
+            op("g", lambda: g.iota(out, pat, base, cm, allow_small_or_imprecise_dtypes=True), [], writes)
+        else:
+            op("g", lambda: g.iota(out, pat, base, cm), [], writes)
+
+    def quant(name, a, b, in_, reads, key):
+        op("v", lambda: V.quantize_mx(T[name + "c"][:, a:b], T[name + "s"][:, a:b], in_), reads, [key + "c", key + "s"])
+
+    def pickc(dst, a, b, src, w, off, rk, ok, wk):
+        op("v", lambda: V.tensor_copy(T[dst + "c"][:, a:b].bitcast(dt.uint32),
+                                      T[src + "c"][:, 0:w].bitcast(dt.uint32).indirect(off)),
+           [k + "c" for k in rk] + [ok], [wk + "c"])
+
+    def picks(dst, a, b, src, w, off, rk, ok, wk):
+        act(T[dst + "s"][:, a:b], T[src + "s"][:, 0:w].indirect(off), Act.Copy, [k + "s" for k in rk] + [ok], [wk + "s"])
+
+    def pick(*a):
+        pickc(*a)
+        picks(*a)
+
+    def bank(i, n):
+        return T.ps[:, 512 * i:512 * i + n]
+
+    def mm(i, ln, la, rn, ra, rb, start, stop, keys):
+        rd = []
+        for k in keys:
+            rd += [k + "c", k + "s"]
+        op("p", lambda: g.tensor.matmul_mx(bank(i, rb - ra), T[ln + "c"][:, la:la + 128], T[ln + "s"][:, la:la + 128],
+                                           T[rn + "c"][:, ra:rb], T[rn + "s"][:, ra:rb], start, stop), rd, ["b%d" % i])
+
+    masks = [_masks(T, topo, h) for h in range(n_ranks)]
+    sent = [0]
+
+    def send(t):
+        for part, sfx in ((0, "c"), (1, "s")):
+            need("g", ["m%d%s" % (t, sfx)], [])
+            trs = []
+            for h in sorted(masks[r]):
+                rid, pid, _ = topo.addr(T.cores[h])
+                src = T["mc%d%s" % (t, sfx)][:, PAIR * h:PAIR * h + PAIR]
+                dst = T["land%d%s" % (t, sfx)][:, PAIR * r:PAIR * r + PAIR]
+                if part == 0:
+                    src, dst = src.bitcast(dt.uint8), dst.bitcast(dt.uint8)
+                es = masks[r][h][part]
+                sent[0] += len(es)
+                trs.append(RemoteDMATransfer(dst_ids=[DstId(rid=rid, pnc=pid)], dma_engine_mask=sum(1 << e for e in es),
+                                             remote_sem=T.sem["arr%s%d" % (sfx, t)], src=src, dst=dst))
+            g.remote_dma_fused(trs, local_sem=T.sem.sent)
+            total = sum(len(masks[h][r][part]) for h in range(n_ranks) if h != r)
+            count["arr%s%d" % (sfx, t)] = total
+            lastw["land%d%s" % (t, sfx)] = ("arr%s%d" % (sfx, t), total)
+        count["sent"] = sent[0]
+        lastw["sent"] = ("sent", sent[0])
+
+    c0 = 2 * ((PAIR * r) // 32)
+    nown = -(-((PAIR * r) % 32 + PAIR) // 16)
+    lw = E + 16 * nown
+    shift = float(E - 16 * c0)
+    kbase = 69632.0
+
+    for k in range(4):
+        dma("s" if k % 2 == 0 else "a", T.wr[32 * k:32 * k + 32, 0:6], T.rev[:], "ldr", [], ["wr%d" % k])
+    lastw["wr"] = ("ldr", count["ldr"])
+    dma("s", T.mt[:], T.m[:], "ldm", [], ["mt"])
+    dma("s", T.bt[:, 0:E], T.b[:], "ldb", [], ["bt0"])
+    dma("s", T.ut[:], T.u[:], "ldu", [], ["ut"])
+    dma("s", T.wt[:], T.w[:], "ldw", [], ["wt"])
+
+    iota(T.pint[:, 0:1], [[0, 1]], 0, 1, ["pint"], small=False)
+    iota(T.blf[:], [[1, 6], [0, 2]], 0, 0, ["blf"])
+    iota(T.econ[:], [[16, 6], [0, 32]], 0, 0, ["econ"])
+    iota(T.sm[:, 0:2], [[64, 2]], 0, 1, ["slot"])
+    for k in range(2):
+        iota(T.src0[:, 96 * k:96 * k + 96], [[16, 6], [1, 8], [96, 2]], 0, 0, ["src0%d" % k])
+    fill(T.ones[:], 1.0, ["ones"])
+    fill(T.swin[:], 0.0, ["swin"])
+    fill(T.cmp[:, E:2 * 208:208], -191.0, ["cmpx"])
+    fill(T.sw[:], 0, ["sw"])
+    p_ = T.pint[:, 0:1]
+    ts(T.pi2[:, 5:6], p_, 1, None, Op.bitwise_and, None, ["pint"], ["pi5"])
+    ts(T.pi2[:, 6:7], p_, 1, None, Op.arith_shift_right, None, ["pint"], ["pi6"])
+    ts(T.pi2[:, 0:1], p_, 4, 1, Op.arith_shift_right, Op.bitwise_and, ["pint"], ["pi0"])
+    ts(T.pi2[:, 1:2], p_, 16, 1, Op.bitwise_and, Op.arith_shift_right, ["pint"], ["pi1"])
+    ts(T.pi2[:, 2:3], p_, 15, None, Op.bitwise_and, None, ["pint"], ["pi2"])
+    ts(T.pi2[:, 3:4], p_, 4, None, Op.arith_shift_right, None, ["pint"], ["pi3"])
+    ts(T.pi2[:, 4:5], p_, 14, None, Op.bitwise_and, None, ["pint"], ["pi4"])
+    ts(T.pi2[:, 7:8], p_, 31, None, Op.bitwise_and, None, ["pint"], ["pi7"])
+    cp(T.bl[:], T.blf[:], ["blf"], ["bl"])
+    cp(T.pc[:, 0:8], T.pi2[:, 0:8], ["pi%d" % k for k in range(8)], ["pc"])
+    odd, odd8, pm16, grp, pm14, pm2, phalf, pm32 = [T.pc[:, k:k + 1] for k in range(8)]
+    fill(T.wsel[:], 0.0, ["wsel"])
+    ts(T.sm[:, 10:11], pm2, 96.0, phalf, Op.mult, Op.add, ["pc"], ["cole"])
+    fill(T.etp[:], 0.0, ["etp"])
+    act(T.econ[:], T.econ[:], Act.Identity, ["cole"], ["econ"], bias=T.sm[:, 10:11])
+    op("g", lambda: g.affine_select(T.ident[:], T.ones[:], [[-1, 128]], Op.is_equal, 0.0, 0, 1), ["ones"], ["ident"])
+    iota(T.c16[:], [[16, 12]], 0, 0, ["c16"])
+    iota(T.n48[:], [[1, 48]], 0, 0, ["n48"])
+    ts(T.qi[:, 0:2], T.sm[:, 0:2], 1.0 / 48, 136.0 - 23.5 / 48, Op.mult, Op.add, ["slot"], ["qi"])
+    fill(T.bt[:, E:512], 0.0, ["bt1"])
+    ts(T.sm[:, 2:4], T.qi[:, 0:2], 136.0, 48.0, Op.subtract, Op.mult, ["qi"], ["sbase"])
+    act(T.src[:], T.src0[:], Act.Identity, ["src00", "src01", "pc"], ["src"], bias=odd8)
+    act(T.xt[:], T.wsel[:], Act.Copy, ["wsel"], ["xt0", "xt1"])
+
+    ts(T.hb[:, 0:6], T.wr[:, 0:6], 512.0 / E, kbase - 95.5 * 512.0 / E, Op.mult, Op.add, ["wr"], ["hb"])
+    tt(T.kb[:], T.hb[:, 0:6].indirect(T.bl[:]), T.econ[:], Op.add, ["hb", "bl", "econ"], ["kb"])
+    tr(T.krow[:], T.kb[:], ["kb"], ["krow"])
+    cp(T.revf[:, 0:6], T.wr[:, 0:6], ["wr"], ["revf"])
+
+    def rank_a(row, col, x, b, j, rk, wk):
+        act(T.junk[:, E * j:E * j + E], row, Act.Sign, rk, [wk], bias=col[:, 32 * b:32 * b + 1], scale=-1.0,
+            accum_out=x[:, b:b + 1])
+
+    for b in range(4):
+        rank_a(T.krow[:], T.kb, T.xk, b, b, ["krow", "kb"], "xk%d" % b)
+    for b in (4, 5):
+        o = 208 * (b - 4)
+        ts(T.cmp[:, o:o + E], T.krow[:], T.kb[:, 32 * b:32 * b + 1], 2.0, Op.is_lt, Op.mult, ["krow", "kb"], ["cmp%d" % b])
+    for b in (4, 5):
+        o = 208 * (b - 4)
+        op("v", lambda: V.tensor_reduce(T.xk[:, b:b + 1], T.cmp[:, o:o + E + 1], AxisListType.X, Op.add),
+           ["cmp%d" % b, "cmpx"], ["xk%d" % b])
+    quant("q0", 0, E, T.mt[:], ["mt"], "q0")
+    act(T.revb[:], T.revf[:, 0:6].indirect(T.bl[:]), Act.Copy, ["revf", "bl"], ["revb"])
+    act(T.etp[:, 3:515:4], T.ident[:], Act.Copy, ["ident"], ["etp"])
+    act(T.etn[:, 0:516], T.etp[:, 0:516], Act.Copy, ["etp"], ["etn"], scale=-1.0)
+    act(T.base[:], T.c16[:], Act.Identity, ["c16", "pc"], ["base"], bias=pm16)
+    xk = ["xk%d" % b for b in range(6)]
+    xr = ["xr%d" % b for b in range(6)]
+    ts(T.hi2[:, 0:6], T.xk[:, 0:6], 191.0 - 15.0 + 4608.0, None, Op.add, None, xk, ["hi2"])
+    tt(T.q2[:, 0:6], T.hi2[:, 0:6], T.xk[:, 0:6], Op.add, ["hi2"] + xk, ["q2"])
+    ts(T.qoff[:, 0:6], T.q2[:, 0:6], 4608.0 - 191.0, 0.5, Op.subtract, Op.mult, ["q2"], ["qoff0"])
+    ts(T.qoff[:, 6:12], T.q2[:, 0:6], 4608.0 - 191.0 - 32.0, 0.5, Op.subtract, Op.mult, ["q2"], ["qoff1"])
+    cp(T.swin[:].indirect(T.qoff[:]), T.src[:], ["qoff0", "qoff1", "src"], ["swin"])
+    tr(T.swt[:], T.swin[:], ["swin"], ["swt"])
+    tt(T.sw[:, 0:12], T.swt[:, 0:2 * E:32], T.swt[:, 16:2 * E:32], Op.add, ["swt"], ["sw"])
+    cp(T.soff[:], T.sw[:, 0:12], ["sw"], ["soff"])
+    pick("mc0", 0, E, "q0", E, T.soff[:], ["q0"], "soff", "m0")
+    send(0)
+
+    iota(T.i16[:], [[0, 8], [1, 16]], 0, 0, ["i16"])
+    iota(T.cc[:, 0:8], [[1, 8]], 0, 0, ["cc0"])
+    iota(T.cc[:, 8:12], [[1, 4]], 4, 0, ["cc1"])
+    iota(T.c2[:], [[1, 2], [64, 3], [0, 2]], 0, 0, ["c2"])
+    tr(T.rrow[:], T.revb[:], ["revb"], ["rrow"])
+    for b in range(6):
+        rank_a(T.rrow[:], T.revb, T.xr, b, 4 + b, ["rrow", "revb"], "xr%d" % b)
+    lo = kbase + 512.0 * r
+    kcol = T.kb[:, 0:E:32]
+    ts(T.list16[:, 0:1], pm14, odd, None, Op.add, None, ["pc"], ["list16"])
+    ts(T.lt[:, 8:14], kcol, lo, shift, Op.is_ge, Op.mult, ["kb"], ["lt1"])
+    ts(T.lt[:, 16:22], kcol, lo + 512.0, shift, Op.is_ge, Op.mult, ["kb"], ["lt2"])
+    cp(T.sd[:], T.sw[:].indirect(T.list16[:, 0:1]), ["sw", "list16"], ["sd"])
+    tt(T.lt[:, 24:30], T.lt[:, 8:14], T.lt[:, 16:22], Op.subtract, ["lt1", "lt2"], ["lt3"])
+    ts(T.fi[:, 0:12], T.sd[:, 0:12], 252, None, Op.bitwise_and, None, ["sd"], ["fb"])
+    ts(T.fi[:, 12:24], T.sd[:, 0:12], 3, None, Op.bitwise_and, None, ["sd"], ["fj"])
+    ts(T.ff[:, 48:60], T.sd[:, 0:12], 96.0, -95.5, Op.is_ge, Op.mult, ["sd"], ["fg"])
+    for k in range(3):
+        ts(T.fi[:, 24 + 12 * k:36 + 12 * k], T.fi[:, 12:24], float(k + 1), float(k), Op.is_lt, Op.add, ["fj"], ["ft%d" % k])
+    tt(T.ff[:, 36:48], T.fi[:, 0:12], T.ff[:, 48:60], Op.add, ["fb", "fg"], ["fh"])
+    quant("qb", 0, 128, T.bt[:], ["bt0", "bt1"], "qb")
+    for k in range(3):
+        tt(T.ff[:, 12 * k:12 * k + 12], T.fi[:, 24 + 12 * k:36 + 12 * k], T.ff[:, 36:48], Op.add, ["ft%d" % k, "fh"],
+           ["ff%d" % k])
+    ts(T.fi[:, 0:12], T.sw[:, 0:12], 2, None, Op.arith_shift_right, None, ["sw"], ["fb"])
+    ts(T.foff[:], T.ff[:, 0:36], 2.0, None, Op.mult, None, ["ff0", "ff1", "ff2"], ["foff"])
+    cp(T.boff[:], T.fi[:, 0:12], ["fb"], ["boff"])
+    fill(T.zoff[:], 0, ["zoff"])
+    ts(T.lt[:, 0:6], T.xr[:, 0:6], 0.5, 95.5, Op.mult, Op.add, xr, ["lt0"])
+    fill(T.rst[:], 1.0, ["rst"])
+    tt(T.l32[:, 0:6], T.lt[:, 0:6], T.lt[:, 24:30], Op.add, ["lt0", "lt3"], ["l32"])
+    act(T.lb[:], T.l32[:, 0:6].indirect(T.bl[:]), Act.Copy, ["l32", "bl"], ["lb"])
+    for b in range(3):
+        quant("ep", 128 * b, 128 * b + 128, T.etp[:, 3 - b:515 - b], ["etp"], "ep%d" % b)
+    tr(T.lrow[:], T.lb[:], ["lb"], ["lrow"])
+    act(T.ag[:], T.lrow[:].indirect(T.foff[:]), Act.Copy, ["lrow", "foff"], ["ag"])
+    quant("ep", 384, 512, T.etp[:, 0:512], ["etp"], "ep3")
+    for b in range(4):
+        quant("en", 128 * b, 128 * b + 128, T.etn[:, 3 - b:515 - b], ["etn"], "en%d" % b)
+    for b in range(4):
+        mm(4 + b, "en", 128 * b, "mc0", 0, E, True, False, ["en%d" % b, "m0"])
+    pick("land0", E, lw, "q0", E, T.soff[:, c0:c0 + nown], ["q0"], "soff", "own0")
+    quant("qu", 0, 128, T.ut[:], ["ut"], "qu")
+    tr(T.agt[:], T.ag[:], ["ag"], ["agt"])
+    pick("bx", 0, E, "qb", 128, T.boff[:], ["qb"], "boff", "bx")
+    cp(T.aoff[:], T.agt[:, 0:3 * E:16], ["agt"], ["aoff"])
+    for b in range(4):
+        mm(b, "ep", 128 * b, "bx", 0, E, True, False, ["ep%d" % b, "bx"])
+    tt(T.sm[:, 4:6], T.sm[:, 0:2], T.sm[:, 2:4], Op.subtract, ["slot", "sbase"], ["sown"])
+    ts(T.sm[:, 6:8], T.sm[:, 2:4], pm16, None, Op.add, None, ["sbase", "pc"], ["sbp"])
+    ts(T.sm[:, 16:64], T.n48[:], float(PAIR), None, Op.is_ge, None, ["n48"], ["ge24"])
+    ts(T.sm[:, 8:10], T.sm[:, 4:6], float(PAIR), None, Op.is_ge, None, ["sown"], ["sfl"])
+
+    def tables(step):
+        if step == 0:
+            picks("ur", 0, 128, "qu", 128, T.zoff[:], ["qu"], "zoff", "ur")
+            for x in range(2):
+                ts(T.cl[:, 4 * x:4 * x + 3], T.c16[:, 0:3], T.sm[:, 6 + x:7 + x], None, Op.add, None, ["c16", "sbp"],
+                   ["cl%d" % x])
+                ts(T.t1[:, 48 * x:48 * x + 48], T.n48[:], T.sm[:, 4 + x:5 + x], -1e-33, Op.is_lt, Op.mult, ["n48", "sown"],
+                   ["t1%d" % x])
+                ts(T.t2[:, 48 * x:48 * x + 48], T.sm[:, 16:64], T.sm[:, 8 + x:9 + x], 1e29, Op.not_equal, Op.mult,
+                   ["ge24", "sfl"], ["t2%d" % x])
+            fill(T.rst[:, 0:96:48], 0.0, ["rst"])
+            tt(T.thr[:], T.t1[:], T.t2[:], Op.add, ["t10", "t11", "t20", "t21"], ["thr"])
+        elif step == 1:
+            pickc("ur", 0, 128, "qu", 128, T.zoff[:], ["qu"], "zoff", "ur")
+            ts(T.k8[:], T.cc[:], grp, float(CAP), Op.is_equal, Op.mult, ["cc0", "cc1", "pc"], ["k8"])
+        else:
+            ts(T.wsel[:, 0:512:4], T.i16[:], pm16, None, Op.is_equal, None, ["i16", "pc"], ["wsel"])
+            quant("wq", 0, 128, T.wsel[:], ["wsel"], "wq")
+
+    def one_round(t):
+        land, an, mc = "land%d" % t, "a%d" % t, "mc%d" % t
+        for k in range(3):
+            pick(an, E * k, E * k + E, land, lw, T.aoff[:, 12 * k:12 * k + 12], [land, "own%d" % t], "aoff", "%s%d" % (an, k))
+        if t == 0:
+            tables(0)
+        for k, b in ((0, 0), (0, 1), (0, 2), (0, 3), (1, 0), (1, 1), (2, 0), (2, 1), (1, 2), (2, 2), (1, 3), (2, 3)):
+            mm(b, "ep", 128 * b, an, E * k, E * k + E, False, k == 2, ["ep%d" % b, "%s%d" % (an, k)])
+        for b in range(4):
+            if b % 2 == 0:
+                act(T.zt[:, b:4 * E:4], bank(b, E), Act.Copy, [], ["b%d" % b, "z%d" % b], scale=0.25)
+            else:
+                ts(T.zt[:, b:4 * E:4], bank(b, E), 0.25, None, Op.mult, None, [], ["b%d" % b, "z%d" % b])
+        quant(mc, FAR, FAR + E, T.zt[:], ["z0", "z1", "z2", "z3"], "c%d" % t)
+        if t == 0:
+            tables(1)
+        for b in range(4):
+            mm(4 + b, "ep", 128 * b, mc, FAR, FAR + E, False, True, ["ep%d" % b, "c%d" % t])
+        for b in range(4):
+            if b % 2 == 0:
+                act(T.yt[:, b:4 * E:4], bank(4 + b, E), Act.Copy, [], ["b%d" % (4 + b), "y%d" % b])
+            else:
+                cp(T.yt[:, b:4 * E:4], bank(4 + b, E), [], ["b%d" % (4 + b), "y%d" % b])
+        quant("yq", 0, E, T.yt[:], ["y0", "y1", "y2", "y3"], "yq")
+        if t == 0:
+            tables(2)
+        mm(0, "ur", 0, "yq", 0, E, True, True, ["ur", "yq"])
+        mm(1, "yq", 0, "ur", 0, 128, True, True, ["ur", "yq"])
+        mm(2, "yq", 64, "ur", 0, 128, True, True, ["ur", "yq"])
+        act(T.arow[:], bank(0, E), Act.Abs, [], ["b0", "arow"])
+        for x in range(2):
+            op("v", lambda: V.tensor_reduce(T.ncol[:, x:x + 1], bank(1 + x, 1), AxisListType.X, Op.max, negate=True,
+                                            apply_absolute_value=True), [], ["b%d" % (1 + x), "ncol%d" % x])
+        act(T.dd[:, 0:48], T.arow[:].indirect(T.cl[:, 0:3]), Act.Identity, ["arow", "cl0", "ncol0"], ["dd0"],
+            bias=T.ncol[:, 0:1])
+        ts(T.dd[:, 48:96], T.arow[:].indirect(T.cl[:, 4:7]), T.ncol[:, 1:2], None, Op.add, None, ["arow", "cl1", "ncol1"], ["dd1"])
+        tt(T.beats[:], T.dd[:], T.thr[:], Op.is_gt, ["dd0", "dd1", "thr"], ["beats"])
+        op("v", lambda: V.tensor_tensor_scan(T.cnt[:], T.rst[:], T.beats[:], 0.0, Op.mult, Op.add), ["beats", "rst"], ["cnt"])
+        ts(T.xt[:, 0:32:4], T.k8[:, 0:8], T.cnt[:, 47:48], float(FAR), Op.is_gt, Op.mult, ["k8", "cnt"], ["xt0"])
+        ts(T.xt[:, 32:48:4], T.k8[:, 8:12], T.cnt[:, 95:96], float(FAR), Op.is_gt, Op.mult, ["k8", "cnt"], ["xt1"])
+        quant("xq", 0, 128, T.xt[:], ["xt0", "xt1"], "xq")
+        mm(3, "wq", 0, "xq", 0, 128, True, True, ["wq", "xq"])
+        tt(T.offf[:, 0:12], bank(3, 12), T.base[:], Op.add, ["base"], ["b3", "offf"])
+        cp(T["off%d" % t][:], T.offf[:, 0:12], ["offf"], ["off%d" % t])
+
+    one_round(0)
+    pick("mc1", 0, E, "mc0", FAR + E, T.off0[:], ["m0", "c0"], "off0", "m1")
+    send(1)
+
+    for b in range(4):
+        mm(b, "ep", 128 * b, "bx", 0, E, True, False, ["ep%d" % b, "bx"])
+    pick("land1", E, lw, "mc0", FAR + E, T.off0[:, c0:c0 + nown], ["m0", "c0"], "off0", "own1")
+    ts(T.p32[:, 0:6], T.xk[:, 0:6], 0.5, 95.5, Op.mult, Op.add, xk, ["p32"])
+    ts(T.lt[:, 0:12], T.c2[:], pm32, None, Op.add, None, ["c2", "pc"], ["lt0", "lt1"])
+    for o in range(2):
+        quant("qw", 128 * o, 128 * o + 128, T.wt[:, 512 * o:512 * o + 512], ["wt"], "qw%d" % o)
+    act(T.pb[:], T.p32[:, 0:6].indirect(T.bl[:]), Act.Copy, ["p32", "bl"], ["pb"])
+    ts(T.dupl[:], T.lt[:, 0:12], pm32, None, Op.add, None, ["lt0", "pc"], ["dupl"])
+    fill(T.win0[:, 0:FAR], 0.0, ["win0a"])
+    fill(T.win0[:, FAR:FAR + E], 1.0, ["win0b"])
+    fill(T.win1[:, E:FAR], 0.0, ["win1h"])
+    tr(T.prow[:], T.pb[:], ["pb"], ["prow"])
+    act(T.pd[:], T.prow[:].indirect(T.dupl[:]), Act.Copy, ["prow", "dupl"], ["pd"])
+    cp(T.win1[:, 0:E], T.win0[:].indirect(T.off0[:]), ["win0a", "win0b", "off0"], ["win1a"])
+    tr(T.pdt[:], T.pd[:], ["pd"], ["pdt"])
+    ts(T.win1[:, FAR:FAR + E], T.win1[:, 0:E], 1.0, None, Op.add, None, ["win1a"], ["win1b"])
+    cp(T.poff[:], T.pdt[:, 0:E:16], ["pdt"], ["poff"])
+    for b in (2, 3):
+        mm(4 + b, "en", 128 * b, "mc1", 0, E, True, False, ["en%d" % b, "m1"])
+    pick("m1e", 0, E, "mc1", E, T.poff[:], ["m1"], "poff", "m1e")
+    for o in range(2):
+        mm(4 + o, "qw", 128 * o, "m1e", 0, E, True, True, ["qw%d" % o, "m1e"])
+    cp(T.y0[:, 0:E], bank(4, E), [], ["b4", "y0a"])
+    act(T.y0[:, E:2 * E], bank(5, E), Act.Copy, [], ["b5", "y0b"])
+    for b in (0, 1):
+        mm(4 + b, "en", 128 * b, "mc1", 0, E, True, False, ["en%d" % b, "m1"])
+    dma("s", T.y[:, 0:2 * E], T.y0[:], "sty", ["y0a", "y0b", "sent"], [])
+
+    one_round(1)
+    pick("m2s", 0, E, "mc1", FAR + E, T.off1[:], ["m1", "c1"], "off1", "m2s")
+    pick("m2e", 0, E, "m2s", E, T.poff[:], ["m2s"], "poff", "m2e")
+    for o in range(2):
+        mm(4 + o, "qw", 128 * o, "m2e", 0, E, True, True, ["qw%d" % o, "m2e"])
+    cp(T.ups[:], T.win1[:].indirect(T.off1[:]), ["win1a", "win1b", "win1h", "off1"], ["ups"])
+    dma("s", T.oc[:], T.m2ec[:].bitcast(dt.uint8), "sto", ["m2ec"], [])
+    for k in range(4):
+        dma("s" if k < 2 else "a", T.osc[4 * k:4 * k + 4, :], T.m2es[32 * k:32 * k + 4, :], "sto", ["m2es"], [])
+    cp(T.y1[:, 0:E], bank(4, E), [], ["b4", "y1a"])
+    act(T.y1[:, E:2 * E], bank(5, E), Act.Copy, [], ["b5", "y1b"])
+    cp(T.upe[:], T.ups[:].indirect(T.poff[:]), ["ups", "poff"], ["upe"])
+    dma("s", T.y[:, 2 * E:3 * E], T.y1[:, 0:E], "sto", ["y1a"], [])
+    dma("a", T.y[:, 3 * E:4 * E], T.y1[:, E:2 * E], "sto", ["y1b"], [])
+    dma("s", T.up[:], T.upe[0:1, :], "sto", ["upe"], [])
+
+    for s in SEMAPHORES:
+        if count.get(s, 0) > 0:
+            g.wait_ge(T.sem[s], count[s])

@@ -4,8 +4,11 @@ from concourse.mybir import dt, AluOpType, AxisListType, ActivationFunctionType
 E = 192
 PAIR = 24
 CAP = 8
+BLK = 32
 FAR = 256
 X4 = "float8_e4m3fn_x4"
+XH, XL, XU, XE, XS, XW = 0, 12, 24, 36, 48, 152
+X1 = 160
 
 
 def _sb(n, d):
@@ -13,29 +16,29 @@ def _sb(n, d):
 
 
 SCRATCH = {"ps": ("psum", [128, 4096], "float32")}
-for _n, _w in (("q0", E), ("mc0", FAR + E), ("mc1", FAR + E), ("land0", 240), ("land1", 240), ("a0", 3 * E), ("a1", 3 * E),
-               ("qb", 128), ("bx", E), ("qu", 128), ("ur", 128), ("qw", 256), ("ep", 512), ("en", 512), ("yq", E),
-               ("xq", 128), ("wq", 128), ("m1e", E), ("m2s", E), ("m2e", E)):
+for _n, _w in (("q0", 240), ("mc0", FAR + E), ("m1", E), ("c1", E), ("ld", 2 * FAR), ("nl", FAR), ("a0", 3 * E), ("a1", 3 * E),
+               ("bx", E), ("qu", 128), ("ur", 128), ("qw", 256), ("ep", 512), ("en", 512), ("yq", E),
+               ("xq", X1 + 128), ("wq", 256), ("me", FAR + E), ("mo", E)):
     SCRATCH[_n + "c"] = _sb(_w, X4)
     SCRATCH[_n + "s"] = _sb(_w, "uint8")
-for _n, _w in (("mt", 4 * E), ("bt", 512), ("ut", 512), ("wt", 1024), ("zt", 4 * E), ("yt", 4 * E), ("xt", 512), ("wsel", 512),
-               ("etp", 528), ("etn", 528), ("ones", 128), ("ident", 128), ("hb", 16), ("junk", 10 * E), ("cmp", 2 * 208),
-               ("hi2", 16), ("src0", E), ("src", E), ("swin", 2 * E), ("swt", 2 * E), ("l32", 16), ("p32", 16), ("lb", E),
-               ("lrow", E), ("pb", E), ("prow", E), ("pd", E), ("pdt", E), ("ag", 3 * E), ("agt", 3 * E), ("qi", 16),
-               ("beats", 96), ("rst", 96), ("cnt", 96), ("win0", FAR + E), ("win1", FAR + E), ("ups", E)):
+for _n, _w in (("mt", 960), ("ut", 512), ("wt", 1024), ("zt", 4 * E), ("yt", 4 * E), ("xt", 4 * XW), ("wsel", 4 * XW),
+               ("etp", 528), ("etn", 528), ("hb", 16), ("junk", 10 * E), ("cmp", 2 * E), ("csum", E),
+               ("src0", 96), ("src", 96), ("swin", 224), ("swt", 416), ("lb", E), ("lrow", E),
+               ("ag", 3 * E), ("agt", 3 * E), ("qi", 16), ("hi", 16), ("i16", 128),
+               ("beats", 96), ("rst", 96), ("cnt", 96)):
     SCRATCH[_n] = _sb(_w, "bfloat16")
-for _n, _w in (("pc", 8), ("c2", 12), ("econ", E), ("kb", E), ("krow", E), ("revf", 16), ("revb", E), ("rrow", E), ("xk", 8),
-               ("xr", 8), ("q2", 8), ("sm", 64), ("n48", 48), ("c16", 12), ("base", 12), ("cc", 12), ("k8", 12), ("i16", 128),
-               ("blf", 12), ("thr", 96), ("t2", 96), ("t1", 96), ("arow", E), ("ncol", 8), ("dd", 96), ("offf", 16),
-               ("y0", 2 * E), ("y1", 2 * E), ("upe", E), ("lt", 32), ("ff", 64)):
+for _n, _w in (("erow", E), ("econ", E), ("tin", 96), ("tab", 96), ("kb", E), ("krow", E), ("revf", 16), ("revb", E),
+               ("rrow", E), ("xk", 8), ("xr", 8), ("sm", 64), ("n48", 48), ("c16", 40), ("k8", 80), ("pe", 24),
+               ("blf", 12), ("thr", 96), ("t2", 96), ("t1", 96), ("arow", E), ("ncol", 8), ("dd", 96),
+               ("ya", FAR + E), ("yb", FAR + E), ("yo", 2 * E), ("upo", 16), ("lt", 32), ("l32", 16), ("ff", 64)):
     SCRATCH[_n] = _sb(_w, "float32")
-for _n, _w in (("wr", 16), ("pint", 8), ("pi2", 8), ("sw", 16), ("sd", 16), ("fi", 64)):
+for _n, _w in (("wr", 16), ("sw", 16), ("fi", 64)):
     SCRATCH[_n] = _sb(_w, "int32")
-for _n, _w in (("qoff", 12), ("soff", 12), ("list16", 2), ("foff", 36), ("aoff", 36), ("boff", 12), ("bl", 12),
-               ("dupl", 12), ("poff", 12), ("zoff", 8), ("cl", 8), ("off0", 12), ("off1", 12)):
+for _n, _w in (("qoff", 6), ("soff", 16), ("slist", 2), ("foff", 36), ("aoff", 36), ("boff", 16), ("bl", 12), ("ownl", 2),
+               ("poff", 12), ("moff", 12), ("zoff", 8), ("cl", 8), ("ol", 16), ("lst", 16), ("offe", 12)):
     SCRATCH[_n] = _sb(_w, "uint16")
 
-SEMAPHORES = ["cv", "ca", "cp", "cg", "ldr", "ldm", "ldb", "ldu", "ldw", "sent", "arrc0", "arrs0", "arrc1", "arrs1",
+SEMAPHORES = ["cv", "ca", "cp", "cg", "ldr", "ldm", "ldu", "ldw", "sent", "arrc0", "arrs0", "arrc1", "arrs1", "arrl",
               "sty", "sto"]
 
 Op = AluOpType
@@ -52,12 +55,13 @@ def _masks(T, topo, r):
     ev, od = eng[0::2], eng[1::2]
     codes = [[ev[0]], [ev[1]], [ev[2]], [ev[3]], od[0:2], od[2:4]]
     scales = [ev[0:2], ev[2:4], [od[0]], [od[1]], [od[2]], [od[3]]]
+    lists = [eng[0:2], eng[2:4], eng[4:6], eng[6:8], eng[0:4], eng[4:8]]
     out = {}
     for k, h in enumerate(far):
-        out[h] = (codes[k], scales[k])
+        out[h] = (codes[k], scales[k], lists[k], k // 4)
     for h in near:
         rest = [e for e in topo.engines(me, T.cores[h]) if e not in eng]
-        out[h] = ([rest[0]], [rest[2]])
+        out[h] = ([rest[0]], [rest[2]], [rest[0], rest[2]], 1)
     return out
 
 
@@ -68,7 +72,7 @@ def rank_program(g, core, T, topo):
     n_ranks = len(T.cores)
     eng = {"v": g.vector, "a": g.scalar, "p": g.tensor, "g": g, "s": g.sync}
     own = {"v": "cv", "a": "ca", "p": "cp", "g": "cg"}
-    count = {"cv": 0, "ca": 0, "cp": 0, "cg": 0}
+    count = {"cv": 0, "ca": 0, "cp": 0, "cg": 0, "sent": 0}
     waited = {q: {} for q in eng}
     lastw, readers = {}, {}
 
@@ -131,11 +135,11 @@ def rank_program(g, core, T, topo):
     def tr(out, in_, reads, writes):
         op("v", lambda: V.transpose(out, in_), reads, writes)
 
-    def iota(out, pat, base, cm, writes, small=True):
-        if small:
-            op("g", lambda: g.iota(out, pat, base, cm, allow_small_or_imprecise_dtypes=True), [], writes)
-        else:
-            op("g", lambda: g.iota(out, pat, base, cm), [], writes)
+    def scan(out, d0, d1, o0, reads, writes):
+        op("v", lambda: V.tensor_tensor_scan(out, d0, d1, 0.0, o0, Op.add), reads, writes)
+
+    def iota(out, pat, base, cm, writes):
+        op("g", lambda: g.iota(out, pat, base, cm, allow_small_or_imprecise_dtypes=True), [], writes)
 
     def quant(name, a, b, in_, reads, key):
         op("v", lambda: V.quantize_mx(T[name + "c"][:, a:b], T[name + "s"][:, a:b], in_), reads, [key + "c", key + "s"])
@@ -152,8 +156,8 @@ def rank_program(g, core, T, topo):
         pickc(*a)
         picks(*a)
 
-    def bank(i, n):
-        return T.ps[:, 512 * i:512 * i + n]
+    def bank(i, n, a=0):
+        return T.ps[:, 512 * i + a:512 * i + a + n]
 
     def mm(i, ln, la, rn, ra, rb, start, stop, keys):
         rd = []
@@ -163,82 +167,81 @@ def rank_program(g, core, T, topo):
                                            T[rn + "c"][:, ra:rb], T[rn + "s"][:, ra:rb], start, stop), rd, ["b%d" % i])
 
     masks = [_masks(T, topo, h) for h in range(n_ranks)]
-    sent = [0]
+
+    def remote(hs, part, sides, sem, key):
+        need("g", [key], [])
+        trs = []
+        for h in hs:
+            rid, pid, _ = topo.addr(T.cores[h])
+            src, dst = sides(h)
+            es = masks[r][h][part]
+            count["sent"] += len(es)
+            trs.append(RemoteDMATransfer(dst_ids=[DstId(rid=rid, pnc=pid)], dma_engine_mask=sum(1 << e for e in es),
+                                         remote_sem=T.sem[sem], src=src, dst=dst))
+        g.remote_dma_fused(trs, local_sem=T.sem.sent)
+        count[sem] = sum(len(masks[h][r][part]) for h in range(n_ranks) if h != r)
+        lastw["sent"] = ("sent", count["sent"])
+
+    def block(h):
+        return (r - h) % n_ranks
 
     def send(t):
         for part, sfx in ((0, "c"), (1, "s")):
-            need("g", ["m%d%s" % (t, sfx)], [])
-            trs = []
-            for h in sorted(masks[r]):
-                rid, pid, _ = topo.addr(T.cores[h])
-                src = T["mc%d%s" % (t, sfx)][:, PAIR * h:PAIR * h + PAIR]
-                dst = T["land%d%s" % (t, sfx)][:, PAIR * r:PAIR * r + PAIR]
-                if part == 0:
-                    src, dst = src.bitcast(dt.uint8), dst.bitcast(dt.uint8)
-                es = masks[r][h][part]
-                sent[0] += len(es)
-                trs.append(RemoteDMATransfer(dst_ids=[DstId(rid=rid, pnc=pid)], dma_engine_mask=sum(1 << e for e in es),
-                                             remote_sem=T.sem["arr%s%d" % (sfx, t)], src=src, dst=dst))
-            g.remote_dma_fused(trs, local_sem=T.sem.sent)
-            total = sum(len(masks[h][r][part]) for h in range(n_ranks) if h != r)
-            count["arr%s%d" % (sfx, t)] = total
-            lastw["land%d%s" % (t, sfx)] = ("arr%s%d" % (sfx, t), total)
-        count["sent"] = sent[0]
-        lastw["sent"] = ("sent", sent[0])
+            def sides(h):
+                a, b = FAR * t + PAIR * h, FAR * t + BLK * block(h)
+                src, dst = T["mc0" + sfx][:, a:a + PAIR], T["ld" + sfx][:, b:b + PAIR]
+                return (src.bitcast(dt.uint8), dst.bitcast(dt.uint8)) if part == 0 else (src, dst)
+            sem = "arr%s%d" % (sfx, t)
+            remote(sorted(masks[r]), part, sides, sem, ("m0", "c0")[t] + sfx)
+            lastw["land%d%s" % (t, sfx)] = (sem, count[sem])
 
-    c0 = 2 * ((PAIR * r) // 32)
-    nown = -(-((PAIR * r) % 32 + PAIR) // 16)
-    lw = E + 16 * nown
-    shift = float(E - 16 * c0)
+    def send_lists():
+        for call in range(2):
+            remote([h for h in sorted(masks[r]) if masks[r][h][3] == call], 2,
+                   lambda h: (T.ol[:, 2 * h:2 * h + 2], T.lst[:, 2 * block(h) - 2:2 * block(h)]), "arrl", "ol")
+        lastw["lst"] = ("arrl", count["arrl"])
+
     kbase = 69632.0
+    b16 = 2304.0
 
     for k in range(4):
         dma("s" if k % 2 == 0 else "a", T.wr[32 * k:32 * k + 32, 0:6], T.rev[:], "ldr", [], ["wr%d" % k])
     lastw["wr"] = ("ldr", count["ldr"])
-    dma("s", T.mt[:], T.m[:], "ldm", [], ["mt"])
-    dma("s", T.bt[:, 0:E], T.b[:], "ldb", [], ["bt0"])
+    dma("s", T.mt[:, 0:4 * E], T.m[:], "ldm", [], ["mt0"])
+    dma("a", T.mt[:, 4 * E:960], T.b[:], "ldm", [], ["mt"])
     dma("s", T.ut[:], T.u[:], "ldu", [], ["ut"])
     dma("s", T.wt[:], T.w[:], "ldw", [], ["wt"])
 
-    iota(T.pint[:, 0:1], [[0, 1]], 0, 1, ["pint"], small=False)
+    slot = T.sm[:, 0:2]
     iota(T.blf[:], [[1, 6], [0, 2]], 0, 0, ["blf"])
-    iota(T.econ[:], [[16, 6], [0, 32]], 0, 0, ["econ"])
-    iota(T.sm[:, 0:2], [[64, 2]], 0, 1, ["slot"])
-    for k in range(2):
-        iota(T.src0[:, 96 * k:96 * k + 96], [[16, 6], [1, 8], [96, 2]], 0, 0, ["src0%d" % k])
-    fill(T.ones[:], 1.0, ["ones"])
-    fill(T.swin[:], 0.0, ["swin"])
-    fill(T.cmp[:, E:2 * 208:208], -191.0, ["cmpx"])
-    fill(T.sw[:], 0, ["sw"])
-    p_ = T.pint[:, 0:1]
-    ts(T.pi2[:, 5:6], p_, 1, None, Op.bitwise_and, None, ["pint"], ["pi5"])
-    ts(T.pi2[:, 6:7], p_, 1, None, Op.arith_shift_right, None, ["pint"], ["pi6"])
-    ts(T.pi2[:, 0:1], p_, 4, 1, Op.arith_shift_right, Op.bitwise_and, ["pint"], ["pi0"])
-    ts(T.pi2[:, 1:2], p_, 16, 1, Op.bitwise_and, Op.arith_shift_right, ["pint"], ["pi1"])
-    ts(T.pi2[:, 2:3], p_, 15, None, Op.bitwise_and, None, ["pint"], ["pi2"])
-    ts(T.pi2[:, 3:4], p_, 4, None, Op.arith_shift_right, None, ["pint"], ["pi3"])
-    ts(T.pi2[:, 4:5], p_, 14, None, Op.bitwise_and, None, ["pint"], ["pi4"])
-    ts(T.pi2[:, 7:8], p_, 31, None, Op.bitwise_and, None, ["pint"], ["pi7"])
+    iota(T.erow[:], [[16, 6], [1, 16], [96, 2]], 0, 0, ["erow"])
+    iota(slot, [[64, 2]], 0, 1, ["slot"])
+    iota(T.tin[:, 0:32], [[8, 2], [0, 16]], 0, 0, ["tin0"])
+    iota(T.src0[:], [[16, 6], [1, 8], [96, 2]], 0, 0, ["src0"])
+    iota(T.tin[:, 32:48], [[1, 8], [7, 2]], 0, 0, ["tin1"])
+    iota(T.tin[:, 48:64], [[1, 8], [-6, 2]], 6, 0, ["tin2"])
+    iota(T.tin[:, 64:96], [[0, 2], [1, 16]], 0, 0, ["tin3"])
+    fill(T.wsel[:], 0.0, ["w0", "w1", "w2"])
     cp(T.bl[:], T.blf[:], ["blf"], ["bl"])
-    cp(T.pc[:, 0:8], T.pi2[:, 0:8], ["pi%d" % k for k in range(8)], ["pc"])
-    odd, odd8, pm16, grp, pm14, pm2, phalf, pm32 = [T.pc[:, k:k + 1] for k in range(8)]
-    fill(T.wsel[:], 0.0, ["wsel"])
-    ts(T.sm[:, 10:11], pm2, 96.0, phalf, Op.mult, Op.add, ["pc"], ["cole"])
-    fill(T.etp[:], 0.0, ["etp"])
-    act(T.econ[:], T.econ[:], Act.Identity, ["cole"], ["econ"], bias=T.sm[:, 10:11])
-    op("g", lambda: g.affine_select(T.ident[:], T.ones[:], [[-1, 128]], Op.is_equal, 0.0, 0, 1), ["ones"], ["ident"])
-    iota(T.c16[:], [[16, 12]], 0, 0, ["c16"])
-    iota(T.n48[:], [[1, 48]], 0, 0, ["n48"])
-    ts(T.qi[:, 0:2], T.sm[:, 0:2], 1.0 / 48, 136.0 - 23.5 / 48, Op.mult, Op.add, ["slot"], ["qi"])
-    fill(T.bt[:, E:512], 0.0, ["bt1"])
-    ts(T.sm[:, 2:4], T.qi[:, 0:2], 136.0, 48.0, Op.subtract, Op.mult, ["qi"], ["sbase"])
-    act(T.src[:], T.src0[:], Act.Identity, ["src00", "src01", "pc"], ["src"], bias=odd8)
-    act(T.xt[:], T.wsel[:], Act.Copy, ["wsel"], ["xt0", "xt1"])
+    fill(T.swin[:], 0.0, ["swin"])
+    fill(T.etp[:], 1.0, ["etp"])
+    fill(T.sw[:], 0, ["sw"])
+    act(T.xt[:], T.wsel[:], Act.Copy, ["w0", "w1", "w2"], ["xt0", "xt1", "xtc", "xh00", "xh01", "xh10", "xh11"])
+    tr(T.econ[:], T.erow[:], ["erow"], ["econ"])
+    act(T.qi[:, 0:2], slot, Act.Identity, ["slot"], ["qi"], scale=1.0 / 48, bias=136.0 - 23.5 / 48)
+    act(T.qi[:, 2:4], slot, Act.Identity, ["slot"], ["qh"], scale=1.0 / PAIR, bias=136.0 - 11.5 / PAIR)
+    act(T.pe[:, 1:5:3], slot, Act.Copy, ["slot"], ["pe1"])
+    act(T.sm[:, 2:4], T.qi[:, 0:2], Act.Identity, ["qi"], ["sbase"], scale=48.0, bias=-136.0 * 48)
+    act(T.sm[:, 10:12], T.qi[:, 2:4], Act.Identity, ["qh"], ["h8"], scale=float(BLK - PAIR), bias=-136.0 * (BLK - PAIR))
+    odd8, pm16 = T.tab[:, 0:1], T.tab[:, 64:65]
 
     ts(T.hb[:, 0:6], T.wr[:, 0:6], 512.0 / E, kbase - 95.5 * 512.0 / E, Op.mult, Op.add, ["wr"], ["hb"])
-    tt(T.kb[:], T.hb[:, 0:6].indirect(T.bl[:]), T.econ[:], Op.add, ["hb", "bl", "econ"], ["kb"])
-    tr(T.krow[:], T.kb[:], ["kb"], ["krow"])
     cp(T.revf[:, 0:6], T.wr[:, 0:6], ["wr"], ["revf"])
+    tt(T.kb[:], T.hb[:, 0:6].indirect(T.bl[:]), T.econ[:], Op.add, ["hb", "bl", "econ"], ["kb"])
+    act(T.revb[:], T.revf[:, 0:6].indirect(T.bl[:]), Act.Copy, ["revf", "bl"], ["revb"])
+    tr(T.tab[:, 0:32], T.tin[:, 0:32], ["tin0"], ["tab0"])
+    tr(T.krow[:], T.kb[:], ["kb"], ["krow"])
+    act(T.src[:], T.src0[:], Act.Identity, ["src0", "tab0"], ["src"], bias=odd8)
 
     def rank_a(row, col, x, b, j, rk, wk):
         act(T.junk[:, E * j:E * j + E], row, Act.Sign, rk, [wk], bias=col[:, 32 * b:32 * b + 1], scale=-1.0,
@@ -246,196 +249,258 @@ def rank_program(g, core, T, topo):
 
     for b in range(4):
         rank_a(T.krow[:], T.kb, T.xk, b, b, ["krow", "kb"], "xk%d" % b)
-    for b in (4, 5):
-        o = 208 * (b - 4)
-        ts(T.cmp[:, o:o + E], T.krow[:], T.kb[:, 32 * b:32 * b + 1], 2.0, Op.is_lt, Op.mult, ["krow", "kb"], ["cmp%d" % b])
-    for b in (4, 5):
-        o = 208 * (b - 4)
-        op("v", lambda: V.tensor_reduce(T.xk[:, b:b + 1], T.cmp[:, o:o + E + 1], AxisListType.X, Op.add),
-           ["cmp%d" % b, "cmpx"], ["xk%d" % b])
-    quant("q0", 0, E, T.mt[:], ["mt"], "q0")
-    act(T.revb[:], T.revf[:, 0:6].indirect(T.bl[:]), Act.Copy, ["revf", "bl"], ["revb"])
-    act(T.etp[:, 3:515:4], T.ident[:], Act.Copy, ["ident"], ["etp"])
-    act(T.etn[:, 0:516], T.etp[:, 0:516], Act.Copy, ["etp"], ["etn"], scale=-1.0)
-    act(T.base[:], T.c16[:], Act.Identity, ["c16", "pc"], ["base"], bias=pm16)
-    xk = ["xk%d" % b for b in range(6)]
-    xr = ["xr%d" % b for b in range(6)]
-    ts(T.hi2[:, 0:6], T.xk[:, 0:6], 191.0 - 15.0 + 4608.0, None, Op.add, None, xk, ["hi2"])
-    tt(T.q2[:, 0:6], T.hi2[:, 0:6], T.xk[:, 0:6], Op.add, ["hi2"] + xk, ["q2"])
-    ts(T.qoff[:, 0:6], T.q2[:, 0:6], 4608.0 - 191.0, 0.5, Op.subtract, Op.mult, ["q2"], ["qoff0"])
-    ts(T.qoff[:, 6:12], T.q2[:, 0:6], 4608.0 - 191.0 - 32.0, 0.5, Op.subtract, Op.mult, ["q2"], ["qoff1"])
-    cp(T.swin[:].indirect(T.qoff[:]), T.src[:], ["qoff0", "qoff1", "src"], ["swin"])
-    tr(T.swt[:], T.swin[:], ["swin"], ["swt"])
-    tt(T.sw[:, 0:12], T.swt[:, 0:2 * E:32], T.swt[:, 16:2 * E:32], Op.add, ["swt"], ["sw"])
-    cp(T.soff[:], T.sw[:, 0:12], ["sw"], ["soff"])
-    pick("mc0", 0, E, "q0", E, T.soff[:], ["q0"], "soff", "m0")
-    send(0)
-
-    iota(T.i16[:], [[0, 8], [1, 16]], 0, 0, ["i16"])
-    iota(T.cc[:, 0:8], [[1, 8]], 0, 0, ["cc0"])
-    iota(T.cc[:, 8:12], [[1, 4]], 4, 0, ["cc1"])
-    iota(T.c2[:], [[1, 2], [64, 3], [0, 2]], 0, 0, ["c2"])
+    for x in range(2):
+        ts(T.cmp[:, E * x:E * x + E], T.krow[:], T.kb[:, 128 + 32 * x:129 + 32 * x], None, Op.is_lt, None, ["krow", "kb"],
+           ["cmp%d" % x])
+    for x in range(2):
+        scan(T.csum[:, 96 * x:96 * x + 96], T.cmp[:, E * x:E * x + 96], T.cmp[:, E * x + 96:E * x + E], Op.add,
+             ["cmp%d" % x], ["cs%d" % x])
     tr(T.rrow[:], T.revb[:], ["revb"], ["rrow"])
+    ts(T.qoff[:, 4:6], T.csum[:, 95:E:96], 16.0, None, Op.add, None, ["cs0", "cs1"], ["qoff1"])
+    quant("q0", 0, 240, T.mt[:], ["mt"], "q0")
+    xk = ["xk%d" % b for b in range(4)]
+    xr = ["xr%d" % b for b in range(6)]
     for b in range(6):
         rank_a(T.rrow[:], T.revb, T.xr, b, 4 + b, ["rrow", "revb"], "xr%d" % b)
-    lo = kbase + 512.0 * r
-    kcol = T.kb[:, 0:E:32]
-    ts(T.list16[:, 0:1], pm14, odd, None, Op.add, None, ["pc"], ["list16"])
-    ts(T.lt[:, 8:14], kcol, lo, shift, Op.is_ge, Op.mult, ["kb"], ["lt1"])
-    ts(T.lt[:, 16:22], kcol, lo + 512.0, shift, Op.is_ge, Op.mult, ["kb"], ["lt2"])
-    cp(T.sd[:], T.sw[:].indirect(T.list16[:, 0:1]), ["sw", "list16"], ["sd"])
-    tt(T.lt[:, 24:30], T.lt[:, 8:14], T.lt[:, 16:22], Op.subtract, ["lt1", "lt2"], ["lt3"])
-    ts(T.fi[:, 0:12], T.sd[:, 0:12], 252, None, Op.bitwise_and, None, ["sd"], ["fb"])
-    ts(T.fi[:, 12:24], T.sd[:, 0:12], 3, None, Op.bitwise_and, None, ["sd"], ["fj"])
-    ts(T.ff[:, 48:60], T.sd[:, 0:12], 96.0, -95.5, Op.is_ge, Op.mult, ["sd"], ["fg"])
+    ts(T.qoff[:, 0:4], T.xk[:, 0:4], 0.5, 95.5 + 16.0, Op.mult, Op.add, xk, ["qoff0"])
+    tr(T.tab[:, 32:96], T.tin[:, 32:96], ["tin1", "tin2", "tin3"], ["tab"])
+    cp(T.swin[:].indirect(T.qoff[:]), T.src[:], ["qoff0", "qoff1", "src"], ["swin"])
+    cp(T.slist[:, 0:1], T.tab[:, 32:33], ["tab"], ["slist"])
+    tr(T.swt[:, 0:E], T.swin[:, 16:16 + E], ["swin"], ["swt0"])
+    tr(T.swt[:, E:416], T.swin[:], ["swin"], ["swt1"])
+    ts(T.lt[:, 0:6], T.hb[:, 0:6], 1.0 / 32, 191.0 - kbase / 32 - 2.0 * BLK * r, Op.mult, Op.add, ["hb"], ["lt0"])
+    tt(T.sw[:, 0:13], T.swt[:, 0:416:32], T.swt[:, 16:416:32], Op.add, ["swt0", "swt1"], ["sw"])
+    ts(T.lt[:, 8:14], T.hb[:, 0:6], kbase + 512.0 * r, 2.0 * FAR, Op.is_lt, Op.mult, ["hb"], ["lt1"])
+    cp(T.soff[:], T.sw[:].indirect(T.slist[:, 0:1]), ["sw", "slist"], ["soff"])
+    tt(T.lt[:, 16:22], T.lt[:, 0:6], T.lt[:, 8:14], Op.add, ["lt0", "lt1"], ["lt2"])
+    pick("mc0", 0, E, "q0", E, T.soff[:, 0:12], ["q0"], "soff", "m0")
+
+    op("g", lambda: g.affine_select(T.etp[:], T.etp[:], [[-1, 528]], Op.is_equal, 0.0, 3, 4), [], ["etp"])
+    iota(T.c16[:, 24:40], [[16, 16]], int(b16), 0, ["c16"])
+    iota(T.n48[:], [[1, 48]], 0, 0, ["n48"])
+    send(0)
+    iota(T.c16[:, 0:24], [[0, 2], [16, 12]], int(b16), 0, ["c12"])
+    iota(T.i16[:], [[0, 8], [1, 16]], 0, 0, ["i16", "pool"])
+    iota(T.wsel[0:1, 2:512:4], [[0, 8], [1, 16]], 0, 0, ["w2a"])
+    iota(T.wsel[0:1, 3:512:4], [[0, 128]], 1, 0, ["w2b"])
+
+    def xrow(p, t, a, n, pat, base):
+        iota(T.xt[p:p + 1, 4 * a + t:4 * (a + n):4], pat, base, 0, ["xtc"])
+
+    xrow(0, 2, XE, 12, [[0, 12]], 1)
+    xrow(0, 3, XE, 12, [[16, 12]], 0)
+    xrow(0, 2, XS, 16, [[0, 8], [-1, 2]], 1)
+    if r > 0:
+        xrow(0, 3, XS, 2 * r, [[-BLK, r], [16, 2]], BLK * r)
+    xrow(0, 3, XS + 2 * r, 2, [[16, 2]], 16 * (PAIR * r // 16))
+    if r < n_ranks - 1:
+        xrow(0, 3, XS + 2 * r + 2, 14 - 2 * r, [[-BLK, n_ranks - 1 - r], [16, 2]], BLK * (n_ranks - 1))
+    iota(T.wsel[32:33, 2:512:4], [[0, 16], [1, 8]], 0, 0, ["w2c", "pool"])
+    iota(T.wsel[32:33, 3:512:4], [[0, 128]], 1, 0, ["w2"])
+    xrow(32, 2, XS, 16, [[0, 8], [1, 2]], 0)
+    xrow(32, 3, XS + 2 * r, 2, [[0, 2]], PAIR * r % 16)
+
+    sd = T.sw[:, 0:6]
+    tt(T.l32[:, 0:6], T.xr[:, 0:6], T.lt[:, 16:22], Op.add, xr + ["lt2"], ["l32"])
+    act(T.lb[:], T.l32[:, 0:6].indirect(T.bl[:]), Act.Copy, ["l32", "bl"], ["lb"], scale=0.5)
+    ts(T.fi[:, 8:14], sd, 3, None, Op.bitwise_and, None, ["sw"], ["fj"])
+    ts(T.fi[:, 0:6], sd, 252, None, Op.bitwise_and, None, ["sw"], ["fb"])
+    ts(T.ff[:, 32:38], sd, 96.0, -95.5, Op.is_ge, Op.mult, ["sw"], ["fg"])
+    cp(T.fi[:, 32:48], T.soff[:], ["soff"], ["s32"])
     for k in range(3):
-        ts(T.fi[:, 24 + 12 * k:36 + 12 * k], T.fi[:, 12:24], float(k + 1), float(k), Op.is_lt, Op.add, ["fj"], ["ft%d" % k])
-    tt(T.ff[:, 36:48], T.fi[:, 0:12], T.ff[:, 48:60], Op.add, ["fb", "fg"], ["fh"])
-    quant("qb", 0, 128, T.bt[:], ["bt0", "bt1"], "qb")
+        ts(T.ff[:, 6 * k:6 * k + 6], T.fi[:, 8:14], float(k + 1), float(k), Op.is_lt, Op.add, ["fj"], ["ft%d" % k])
+    tt(T.ff[:, 24:30], T.fi[:, 0:6], T.ff[:, 32:38], Op.add, ["fb", "fg"], ["fh"])
+    ts(T.fi[:, 48:64], T.fi[:, 32:48], 2, None, Op.arith_shift_right, None, ["s32"], ["s4"])
+    ts(T.lt[:, 24:26], T.c16[:, 24:26], pm16, PAIR * r - b16, Op.add, Op.add, ["c16", "tab"], ["lt3"])
     for k in range(3):
-        tt(T.ff[:, 12 * k:12 * k + 12], T.fi[:, 24 + 12 * k:36 + 12 * k], T.ff[:, 36:48], Op.add, ["ft%d" % k, "fh"],
-           ["ff%d" % k])
-    ts(T.fi[:, 0:12], T.sw[:, 0:12], 2, None, Op.arith_shift_right, None, ["sw"], ["fb"])
-    ts(T.foff[:], T.ff[:, 0:36], 2.0, None, Op.mult, None, ["ff0", "ff1", "ff2"], ["foff"])
-    cp(T.boff[:], T.fi[:, 0:12], ["fb"], ["boff"])
-    fill(T.zoff[:], 0, ["zoff"])
-    ts(T.lt[:, 0:6], T.xr[:, 0:6], 0.5, 95.5, Op.mult, Op.add, xr, ["lt0"])
-    fill(T.rst[:], 1.0, ["rst"])
-    tt(T.l32[:, 0:6], T.lt[:, 0:6], T.lt[:, 24:30], Op.add, ["lt0", "lt3"], ["l32"])
-    act(T.lb[:], T.l32[:, 0:6].indirect(T.bl[:]), Act.Copy, ["l32", "bl"], ["lb"])
-    for b in range(3):
-        quant("ep", 128 * b, 128 * b + 128, T.etp[:, 3 - b:515 - b], ["etp"], "ep%d" % b)
+        tt(T.ff[:, 40 + 6 * k:46 + 6 * k], T.ff[:, 6 * k:6 * k + 6], T.ff[:, 24:30], Op.add, ["ft%d" % k, "fh"], ["ff%d" % k])
     tr(T.lrow[:], T.lb[:], ["lb"], ["lrow"])
-    act(T.ag[:], T.lrow[:].indirect(T.foff[:]), Act.Copy, ["lrow", "foff"], ["ag"])
-    quant("ep", 384, 512, T.etp[:, 0:512], ["etp"], "ep3")
+    for x in range(2):
+        ts(T.foff[:, x:36:2], T.ff[:, 40:58], 2.0, None, Op.mult, None, ["ff0", "ff1", "ff2"], ["foff%d" % x])
+    act(T.ag[:], T.lrow[:].indirect(T.foff[:]), Act.Copy, ["lrow", "foff0", "foff1"], ["ag"])
+    ts(T.boff[:], T.fi[:, 48:64], float(E), None, Op.add, None, ["s4"], ["boff"])
+    ts(T.ownl[:], T.lt[:, 24:26], E - 1.0, None, Op.min, None, ["lt3"], ["ownl"])
     for b in range(4):
-        quant("en", 128 * b, 128 * b + 128, T.etn[:, 3 - b:515 - b], ["etn"], "en%d" % b)
-    for b in range(4):
-        mm(4 + b, "en", 128 * b, "mc0", 0, E, True, False, ["en%d" % b, "m0"])
-    pick("land0", E, lw, "q0", E, T.soff[:, c0:c0 + nown], ["q0"], "soff", "own0")
-    quant("qu", 0, 128, T.ut[:], ["ut"], "qu")
+        quant("ep", 128 * b, 128 * b + 128, T.etp[:, 3 - b:515 - b], ["etp"], "ep%d" % b)
+    pick("bx", 0, E, "q0", 240, T.boff[:, 0:12], ["q0"], "boff", "bx")
+    pick("ld", 0, BLK, "mc0", E, T.ownl[:], ["m0"], "ownl", "own0")
     tr(T.agt[:], T.ag[:], ["ag"], ["agt"])
-    pick("bx", 0, E, "qb", 128, T.boff[:], ["qb"], "boff", "bx")
-    cp(T.aoff[:], T.agt[:, 0:3 * E:16], ["agt"], ["aoff"])
+    act(T.etn[:, 0:516], T.etp[:, 0:516], Act.Copy, ["etp"], ["etn"], scale=-1.0)
     for b in range(4):
         mm(b, "ep", 128 * b, "bx", 0, E, True, False, ["ep%d" % b, "bx"])
-    tt(T.sm[:, 4:6], T.sm[:, 0:2], T.sm[:, 2:4], Op.subtract, ["slot", "sbase"], ["sown"])
-    ts(T.sm[:, 6:8], T.sm[:, 2:4], pm16, None, Op.add, None, ["sbase", "pc"], ["sbp"])
+    for q in range(2):
+        cp(T.pe[32 * q:32 * q + 32, 2:3], T.sw[32 * q:32 * q + 32, q:q + 1], ["sw"], ["pa%d" % q])
+    tt(T.pe[:, 0:4:3], slot, T.sm[:, 10:12], Op.add, ["slot", "h8"], ["pe0"])
+    cp(T.aoff[:], T.agt[:, 0:3 * E:16], ["agt"], ["aoff"])
+    for q in range(2, 4):
+        cp(T.pe[32 * q:32 * q + 32, 2:6:3], T.sw[32 * q:32 * q + 32, q:q + 3:2], ["sw"], ["pa%d" % q])
+    fill(T.pe[0:64, 3:6], 300.0, ["pe0", "pe1"])
+    tt(T.sm[:, 4:6], slot, T.sm[:, 2:4], Op.subtract, ["slot", "sbase"], ["sown"])
+    ts(T.sm[:, 6:8], T.sm[:, 2:4], pm16, -b16, Op.add, Op.add, ["sbase", "tab"], ["sbp"])
+    pes = ["pe0", "pe1"] + ["pa%d" % q for q in range(4)]
+    act(T.hi[:, 0:6], T.pe[:, 0:6], Act.Identity, pes, ["hi"], bias=b16 - 7.5)
     ts(T.sm[:, 16:64], T.n48[:], float(PAIR), None, Op.is_ge, None, ["n48"], ["ge24"])
+    fill(T.zoff[:], 0, ["zoff"])
+    fill(T.rst[:], 1.0, ["rst"])
     ts(T.sm[:, 8:10], T.sm[:, 4:6], float(PAIR), None, Op.is_ge, None, ["sown"], ["sfl"])
+    for x in range(2):
+        ts(T.cl[:, 4 * x:4 * x + 3], T.c16[:, 24:27], T.sm[:, 6 + x:7 + x], None, Op.add, None, ["c16", "sbp"], ["cl%d" % x])
+    tt(T.pe[:, 8:14], T.pe[:, 0:6], T.hi[:, 0:6], Op.subtract, pes + ["hi"], ["pd"])
+    act(T.hi[:, 8:10], T.hi[:, 1:5:3], Act.Identity, ["hi"], ["hv"], bias=-b16)
+    act(T.hi[:, 10:12], T.pe[:, 9:13:3], Act.Identity, ["pd"], ["lv"], bias=b16)
+    for x in range(2):
+        for k, (a, n, c) in ((0, (24, 16, 24)), (2, (0, 24, 0))):
+            ts(T.k8[:, 40 * x + a:40 * x + a + n], T.c16[:, c:c + n], T.hi[:, 3 * x + k:3 * x + k + 1], float(CAP),
+               Op.is_equal, Op.mult, ["c16", "c12", "hi"], ["k8%d%d" % (x, k)])
 
-    def tables(step):
-        if step == 0:
-            picks("ur", 0, 128, "qu", 128, T.zoff[:], ["qu"], "zoff", "ur")
+    def wrow(k, x):
+        j = 8 + 2 * k + 3 * x
+        ts(T.wsel[:, x:512:4], T.i16[:], -b16, T.pe[:, j:j + 1], Op.add, Op.is_equal, ["i16", "pd"], ["w%d" % x])
+
+    def wquant(k):
+        quant("wq", 128 * k, 128 * k + 128, T.wsel[:, 0:512], ["w0", "w1", "w2"], "wq%d" % k)
+
+    def digits(x, k):
+        a = (XH, XL)[k]
+        ts(T.xt[:, 4 * a + x:4 * a + 48:4], T.c16[:, 0:12], T.hi[:, 3 * x + 2:3 * x + 3],
+           T.hi[:, 8 + 2 * k + x:9 + 2 * k + x], Op.is_equal, Op.mult, ["c12", "hi", "hv", "lv"], ["xh%d%d" % (x, k)])
+
+    def side(t, step):
+        if (t, step) == (0, 0):
+            wrow(0, 0)
+            wrow(0, 1)
+            for b in range(4):
+                quant("en", 128 * b, 128 * b + 128, T.etn[:, 3 - b:515 - b], ["etn"], "en%d" % b)
+            quant("qu", 0, 128, T.ut[:], ["ut"], "qu")
+            wquant(0)
+        elif (t, step) == (0, 1):
             for x in range(2):
-                ts(T.cl[:, 4 * x:4 * x + 3], T.c16[:, 0:3], T.sm[:, 6 + x:7 + x], None, Op.add, None, ["c16", "sbp"],
-                   ["cl%d" % x])
                 ts(T.t1[:, 48 * x:48 * x + 48], T.n48[:], T.sm[:, 4 + x:5 + x], -1e-33, Op.is_lt, Op.mult, ["n48", "sown"],
                    ["t1%d" % x])
                 ts(T.t2[:, 48 * x:48 * x + 48], T.sm[:, 16:64], T.sm[:, 8 + x:9 + x], 1e29, Op.not_equal, Op.mult,
                    ["ge24", "sfl"], ["t2%d" % x])
+            pick("ur", 0, 128, "qu", 128, T.zoff[:], ["qu"], "zoff", "ur")
+        elif (t, step) == (0, 2):
             fill(T.rst[:, 0:96:48], 0.0, ["rst"])
+        elif (t, step) == (0, 3):
             tt(T.thr[:], T.t1[:], T.t2[:], Op.add, ["t10", "t11", "t20", "t21"], ["thr"])
-        elif step == 1:
-            pickc("ur", 0, 128, "qu", 128, T.zoff[:], ["qu"], "zoff", "ur")
-            ts(T.k8[:], T.cc[:], grp, float(CAP), Op.is_equal, Op.mult, ["cc0", "cc1", "pc"], ["k8"])
-        else:
-            ts(T.wsel[:, 0:512:4], T.i16[:], pm16, None, Op.is_equal, None, ["i16", "pc"], ["wsel"])
-            quant("wq", 0, 128, T.wsel[:], ["wsel"], "wq")
+            digits(0, 0)
+            digits(0, 1)
+        elif (t, step) == (0, 4):
+            digits(1, 0)
+        elif t == 0 and step in (5, 6):
+            wrow(1, step - 5)
+        elif (t, step) == (0, 7):
+            digits(1, 1)
+        elif (t, step) == (0, 8):
+            wquant(1)
+        elif (t, step) == (1, 0):
+            cp(T.ya[:, 0:E], bank(4, E), [], ["b4", "ya0"])
+            act(T.yb[:, 0:E], bank(5, E), Act.Copy, [], ["b5", "yb0"])
+            dma("s", T.y[:, 0:E], T.ya[:, 0:E], "sty", ["ya0", "sent"], [])
+            dma("s", T.y[:, E:2 * E], T.yb[:, 0:E], "sty", ["yb0", "sent"], [])
+            pickc("m1", 0, E, "me", E, T.soff[:, 0:12], ["m1e"], "soff", "m1")
+            cp(T.m1s[:], T.mes[:, 0:E].indirect(T.soff[:, 0:12]), ["m1es", "soff"], ["m1s"])
+        elif (t, step) == (1, 1):
+            pickc("me", FAR, FAR + E, "c1", E, T.poff[:], ["c1"], "poff", "ce")
+        elif (t, step) == (1, 3):
+            picks("me", FAR, FAR + E, "c1", E, T.poff[:], ["c1"], "poff", "ce")
 
     def one_round(t):
-        land, an, mc = "land%d" % t, "a%d" % t, "mc%d" % t
+        land, an = ("ld", "nl")[t], "a%d" % t
+        held, (cand, c0) = ("mc0", "m1")[t], (("mc0", FAR), ("c1", 0))[t]
         for k in range(3):
-            pick(an, E * k, E * k + E, land, lw, T.aoff[:, 12 * k:12 * k + 12], [land, "own%d" % t], "aoff", "%s%d" % (an, k))
-        if t == 0:
-            tables(0)
+            pick(an, E * k, E * k + E, land, FAR, T.aoff[:, 12 * k:12 * k + 12],
+                 [("land0", "nl")[t], "own%d" % t], "aoff", "%s%d" % (an, k))
+        side(t, 0)
         for k, b in ((0, 0), (0, 1), (0, 2), (0, 3), (1, 0), (1, 1), (2, 0), (2, 1), (1, 2), (2, 2), (1, 3), (2, 3)):
             mm(b, "ep", 128 * b, an, E * k, E * k + E, False, k == 2, ["ep%d" % b, "%s%d" % (an, k)])
         for b in range(4):
-            if b % 2 == 0:
-                act(T.zt[:, b:4 * E:4], bank(b, E), Act.Copy, [], ["b%d" % b, "z%d" % b], scale=0.25)
-            else:
-                ts(T.zt[:, b:4 * E:4], bank(b, E), 0.25, None, Op.mult, None, [], ["b%d" % b, "z%d" % b])
-        quant(mc, FAR, FAR + E, T.zt[:], ["z0", "z1", "z2", "z3"], "c%d" % t)
+            mm(4 + b, "en", 128 * b, held, 0, E, True, False, ["en%d" % b, "m%d" % t])
+        for b in range(3):
+            act(T.zt[:, b:4 * E:4], bank(b, E), Act.Copy, [], ["b%d" % b, "z%d" % b], scale=0.25)
+        ts(T.zt[:, 3:4 * E:4], bank(3, E), 0.25, None, Op.mult, None, [], ["b3", "z3"])
+        quant(cand, c0, c0 + E, T.zt[:], ["z0", "z1", "z2", "z3"], "c%d" % t)
         if t == 0:
-            tables(1)
+            send(1)
+        side(t, 1)
         for b in range(4):
-            mm(4 + b, "ep", 128 * b, mc, FAR, FAR + E, False, True, ["ep%d" % b, "c%d" % t])
+            mm(4 + b, "ep", 128 * b, cand, c0, c0 + E, False, True, ["ep%d" % b, "c%d" % t])
         for b in range(4):
             if b % 2 == 0:
                 act(T.yt[:, b:4 * E:4], bank(4 + b, E), Act.Copy, [], ["b%d" % (4 + b), "y%d" % b])
             else:
                 cp(T.yt[:, b:4 * E:4], bank(4 + b, E), [], ["b%d" % (4 + b), "y%d" % b])
+        side(t, 2)
         quant("yq", 0, E, T.yt[:], ["y0", "y1", "y2", "y3"], "yq")
-        if t == 0:
-            tables(2)
+        side(t, 3)
         mm(0, "ur", 0, "yq", 0, E, True, True, ["ur", "yq"])
         mm(1, "yq", 0, "ur", 0, 128, True, True, ["ur", "yq"])
         mm(2, "yq", 64, "ur", 0, 128, True, True, ["ur", "yq"])
+        if t == 1:
+            for o in range(2):
+                mm(4 + o, "qw", 128 * o, "me", FAR, FAR + E, True, True, ["qw%d" % o, "ce"])
+            mm(6, "xq", 0, "wq", 128, 256, True, False, ["xq0", "wq1"])
         act(T.arow[:], bank(0, E), Act.Abs, [], ["b0", "arow"])
         for x in range(2):
             op("v", lambda: V.tensor_reduce(T.ncol[:, x:x + 1], bank(1 + x, 1), AxisListType.X, Op.max, negate=True,
                                             apply_absolute_value=True), [], ["b%d" % (1 + x), "ncol%d" % x])
+        side(t, 4)
         act(T.dd[:, 0:48], T.arow[:].indirect(T.cl[:, 0:3]), Act.Identity, ["arow", "cl0", "ncol0"], ["dd0"],
             bias=T.ncol[:, 0:1])
         ts(T.dd[:, 48:96], T.arow[:].indirect(T.cl[:, 4:7]), T.ncol[:, 1:2], None, Op.add, None, ["arow", "cl1", "ncol1"], ["dd1"])
+        if t == 1:
+            act(T.ya[:, FAR:FAR + E], bank(4, E), Act.Copy, [], ["b4", "yac"])
+            act(T.yb[:, FAR:FAR + E], bank(5, E), Act.Copy, [], ["b5", "ybc"])
+        side(t, 5)
         tt(T.beats[:], T.dd[:], T.thr[:], Op.is_gt, ["dd0", "dd1", "thr"], ["beats"])
-        op("v", lambda: V.tensor_tensor_scan(T.cnt[:], T.rst[:], T.beats[:], 0.0, Op.mult, Op.add), ["beats", "rst"], ["cnt"])
-        ts(T.xt[:, 0:32:4], T.k8[:, 0:8], T.cnt[:, 47:48], float(FAR), Op.is_gt, Op.mult, ["k8", "cnt"], ["xt0"])
-        ts(T.xt[:, 32:48:4], T.k8[:, 8:12], T.cnt[:, 95:96], float(FAR), Op.is_gt, Op.mult, ["k8", "cnt"], ["xt1"])
-        quant("xq", 0, 128, T.xt[:], ["xt0", "xt1"], "xq")
-        mm(3, "wq", 0, "xq", 0, 128, True, True, ["wq", "xq"])
-        tt(T.offf[:, 0:12], bank(3, 12), T.base[:], Op.add, ["base"], ["b3", "offf"])
-        cp(T["off%d" % t][:], T.offf[:, 0:12], ["offf"], ["off%d" % t])
+        side(t, 6)
+        scan(T.cnt[:], T.rst[:], T.beats[:], Op.mult, ["beats", "rst"], ["cnt"])
+        side(t, 7)
+        n = (40, 24)[t]
+        for x in range(2):
+            ts(T.xt[:, 4 * XU + x:4 * (XU + n):4], T.k8[:, 40 * x:40 * x + n], T.cnt[:, 48 * x + 47:48 * x + 48], float(FAR),
+               Op.is_gt, Op.mult, ["k8%d0" % x, "k8%d2" % x, "cnt"], ["xt%d" % x])
+        w = (XW, 128)[t]
+        quant("xq", X1 * t, X1 * t + w, T.xt[:, 0:4 * w], ["xt0", "xt1", "xtc", "xh00", "xh01", "xh10", "xh11"], "xq%d" % t)
+        side(t, 8)
+        mm(3, "wq", 128 * t, "xq", X1 * t, X1 * t + 128, True, True, ["wq%d" % t, "xq%d" % t])
 
     one_round(0)
-    pick("mc1", 0, E, "mc0", FAR + E, T.off0[:], ["m0", "c0"], "off0", "m1")
-    send(1)
+    cp(T.ol[:], bank(3, 16, XS), [], ["b3", "ol"])
+    send_lists()
 
+    for k in range(3):
+        mm(6, "wq", 128, "xq", 12 * k, 12 * k + 128, k == 0, k == 2, ["wq1", "xq0"])
+    for k in range(2):
+        mm(5, "wq", 128, "xq", 12 * k, 12 * k + 128, k == 0, k == 1, ["wq1", "xq0"])
+    fill(T.ya[:, E:FAR], 0.0, ["yag"])
+    fill(T.yb[:, E:FAR], 0.0, ["ybg"])
+    pick("nl", 0, BLK, "mc0", FAR + E, T.ol[:, 2 * r:2 * r + 2], ["m0", "c0"], "ol", "own1")
     for b in range(4):
         mm(b, "ep", 128 * b, "bx", 0, E, True, False, ["ep%d" % b, "bx"])
-    pick("land1", E, lw, "mc0", FAR + E, T.off0[:, c0:c0 + nown], ["m0", "c0"], "off0", "own1")
-    ts(T.p32[:, 0:6], T.xk[:, 0:6], 0.5, 95.5, Op.mult, Op.add, xk, ["p32"])
-    ts(T.lt[:, 0:12], T.c2[:], pm32, None, Op.add, None, ["c2", "pc"], ["lt0", "lt1"])
+    cp(T.moff[:], bank(6, 12), [], ["b6", "moff"])
     for o in range(2):
         quant("qw", 128 * o, 128 * o + 128, T.wt[:, 512 * o:512 * o + 512], ["wt"], "qw%d" % o)
-    act(T.pb[:], T.p32[:, 0:6].indirect(T.bl[:]), Act.Copy, ["p32", "bl"], ["pb"])
-    ts(T.dupl[:], T.lt[:, 0:12], pm32, None, Op.add, None, ["lt0", "pc"], ["dupl"])
-    fill(T.win0[:, 0:FAR], 0.0, ["win0a"])
-    fill(T.win0[:, FAR:FAR + E], 1.0, ["win0b"])
-    fill(T.win1[:, E:FAR], 0.0, ["win1h"])
-    tr(T.prow[:], T.pb[:], ["pb"], ["prow"])
-    act(T.pd[:], T.prow[:].indirect(T.dupl[:]), Act.Copy, ["prow", "dupl"], ["pd"])
-    cp(T.win1[:, 0:E], T.win0[:].indirect(T.off0[:]), ["win0a", "win0b", "off0"], ["win1a"])
-    tr(T.pdt[:], T.pd[:], ["pd"], ["pdt"])
-    ts(T.win1[:, FAR:FAR + E], T.win1[:, 0:E], 1.0, None, Op.add, None, ["win1a"], ["win1b"])
-    cp(T.poff[:], T.pdt[:, 0:E:16], ["pdt"], ["poff"])
-    for b in (2, 3):
-        mm(4 + b, "en", 128 * b, "mc1", 0, E, True, False, ["en%d" % b, "m1"])
-    pick("m1e", 0, E, "mc1", E, T.poff[:], ["m1"], "poff", "m1e")
+    pick("me", 0, E, "mc0", FAR + E, T.moff[:], ["m0", "c0"], "moff", "m1e")
+    cp(T.poff[:], bank(5, 12), [], ["b5", "poff"])
     for o in range(2):
-        mm(4 + o, "qw", 128 * o, "m1e", 0, E, True, True, ["qw%d" % o, "m1e"])
-    cp(T.y0[:, 0:E], bank(4, E), [], ["b4", "y0a"])
-    act(T.y0[:, E:2 * E], bank(5, E), Act.Copy, [], ["b5", "y0b"])
-    for b in (0, 1):
-        mm(4 + b, "en", 128 * b, "mc1", 0, E, True, False, ["en%d" % b, "m1"])
-    dma("s", T.y[:, 0:2 * E], T.y0[:], "sty", ["y0a", "y0b", "sent"], [])
+        mm(4 + o, "qw", 128 * o, "me", 0, E, True, True, ["qw%d" % o, "m1e"])
 
+    pick("nl", BLK, FAR, "ld", 2 * FAR, T.lst[:, 0:14], ["land0", "land1", "own0"], "lst", "nl")
     one_round(1)
-    pick("m2s", 0, E, "mc1", FAR + E, T.off1[:], ["m1", "c1"], "off1", "m2s")
-    pick("m2e", 0, E, "m2s", E, T.poff[:], ["m2s"], "poff", "m2e")
-    for o in range(2):
-        mm(4 + o, "qw", 128 * o, "m2e", 0, E, True, True, ["qw%d" % o, "m2e"])
-    cp(T.ups[:], T.win1[:].indirect(T.off1[:]), ["win1a", "win1b", "win1h", "off1"], ["ups"])
-    dma("s", T.oc[:], T.m2ec[:].bitcast(dt.uint8), "sto", ["m2ec"], [])
+    cp(T.offe[:], bank(3, 12, XE), [], ["b3", "offe"])
+    mm(6, "xq", X1, "wq", 128, 256, False, True, ["xq1", "wq1"])
+    cp(T.yo[:, 0:E], T.ya[:].indirect(T.offe[:]), ["ya0", "yag", "yac", "offe"], ["yo0"])
+    act(T.yo[:, E:2 * E], T.yb[:].indirect(T.offe[:]), Act.Copy, ["yb0", "ybg", "ybc", "offe"], ["yo1"])
+    pick("mo", 0, E, "me", FAR + E, T.offe[:], ["m1e", "ce"], "offe", "mo")
+    ts(T.upo[0:64, :], T.ps[0:64, 3072:3088], 1.0 / FAR, None, Op.mult, None, [], ["b6", "upo"])
+    dma("s", T.y[:, 2 * E:3 * E], T.yo[:, 0:E], "sto", ["yo0"], [])
+    dma("s", T.y[:, 3 * E:4 * E], T.yo[:, E:2 * E], "sto", ["yo1"], [])
+    dma("s", T.oc[:], T.moc[:].bitcast(dt.uint8), "sto", ["moc"], [])
     for k in range(4):
-        dma("s" if k < 2 else "a", T.osc[4 * k:4 * k + 4, :], T.m2es[32 * k:32 * k + 4, :], "sto", ["m2es"], [])
-    cp(T.y1[:, 0:E], bank(4, E), [], ["b4", "y1a"])
-    act(T.y1[:, E:2 * E], bank(5, E), Act.Copy, [], ["b5", "y1b"])
-    cp(T.upe[:], T.ups[:].indirect(T.poff[:]), ["ups", "poff"], ["upe"])
-    dma("s", T.y[:, 2 * E:3 * E], T.y1[:, 0:E], "sto", ["y1a"], [])
-    dma("a", T.y[:, 3 * E:4 * E], T.y1[:, E:2 * E], "sto", ["y1b"], [])
-    dma("s", T.up[:], T.upe[0:1, :], "sto", ["upe"], [])
+        dma("s" if k == 0 else "a", T.osc[4 * k:4 * k + 4, :], T.mos[32 * k:32 * k + 4, :], "sto", ["mos"], [])
+    dma("s", T.up[:], T.upo[XU:XU + 12, :], "sto", ["upo"], [])
 
     for s in SEMAPHORES:
         if count.get(s, 0) > 0:

from concourse.bass import DstId, RemoteDMATransfer
from concourse.mybir import dt, AluOpType, AxisListType, ActivationFunctionType

E = 192
PAIR = 24
CAP = 8
BLK = 32
FAR = 256
X4 = "float8_e4m3fn_x4"
XH, XL, XU, XE, XS, XW = 0, 12, 24, 36, 48, 152
X1 = 160


def _sb(n, d):
    return ("sbuf", [128, n], d)


SCRATCH = {"ps": ("psum", [128, 4096], "float32")}
for _n, _w in (("q0", 240), ("mc0", FAR + E), ("m1", E), ("c1", E), ("ld", 2 * FAR), ("nl", FAR), ("a0", 3 * E), ("a1", 3 * E),
               ("bx", E), ("qu", 128), ("ur", 128), ("qw", 256), ("ep", 512), ("en", 512), ("yq", E),
               ("xq", X1 + 128), ("wq", 256), ("me", FAR + E), ("mo", E)):
    SCRATCH[_n + "c"] = _sb(_w, X4)
    SCRATCH[_n + "s"] = _sb(_w, "uint8")
for _n, _w in (("mt", 960), ("ut", 512), ("wt", 1024), ("zt", 4 * E), ("yt", 4 * E), ("xt", 4 * XW), ("wsel", 4 * XW),
               ("etp", 528), ("etn", 528), ("hb", 16), ("junk", 10 * E), ("cmp", 2 * E), ("csum", E),
               ("src0", 96), ("src", 96), ("swin", 224), ("swt", 416), ("lb", E), ("lrow", E),
               ("ag", 3 * E), ("agt", 3 * E), ("qi", 16), ("hi", 16), ("i16", 128),
               ("beats", 96), ("rst", 96), ("cnt", 96)):
    SCRATCH[_n] = _sb(_w, "bfloat16")
for _n, _w in (("erow", E), ("econ", E), ("tin", 96), ("tab", 96), ("kb", E), ("krow", E), ("revf", 16), ("revb", E),
               ("rrow", E), ("xk", 8), ("xr", 8), ("sm", 64), ("n48", 48), ("c16", 40), ("k8", 80), ("pe", 24),
               ("blf", 12), ("thr", 96), ("t2", 96), ("t1", 96), ("arow", E), ("ncol", 8), ("dd", 96),
               ("ya", FAR + E), ("yb", FAR + E), ("yo", 2 * E), ("upo", 16), ("lt", 32), ("l32", 16), ("ff", 64)):
    SCRATCH[_n] = _sb(_w, "float32")
for _n, _w in (("wr", 16), ("sw", 16), ("fi", 64)):
    SCRATCH[_n] = _sb(_w, "int32")
for _n, _w in (("qoff", 6), ("soff", 16), ("slist", 2), ("foff", 36), ("aoff", 36), ("boff", 16), ("bl", 12), ("ownl", 2),
               ("poff", 12), ("moff", 12), ("zoff", 8), ("cl", 8), ("ol", 16), ("lst", 16), ("offe", 12)):
    SCRATCH[_n] = _sb(_w, "uint16")

SEMAPHORES = ["cv", "ca", "cp", "cg", "ldr", "ldm", "ldu", "ldw", "sent", "arrc0", "arrs0", "arrc1", "arrs1", "arrl",
              "sty", "sto"]

Op = AluOpType
Act = ActivationFunctionType


def _masks(T, topo, r):
    n = len(T.cores)
    me = T.cores[r]
    order = [(r + k) % n for k in range(1, n)]
    far = [h for h in order if topo.chip(T.cores[h]) != topo.chip(me)]
    near = [h for h in order if topo.chip(T.cores[h]) == topo.chip(me)]
    eng = topo.engines(me, T.cores[far[0]])
    ev, od = eng[0::2], eng[1::2]
    codes = [[ev[0]], [ev[1]], [ev[2]], [ev[3]], od[0:2], od[2:4]]
    scales = [ev[0:2], ev[2:4], [od[0]], [od[1]], [od[2]], [od[3]]]
    lists = [eng[0:2], eng[2:4], eng[4:6], eng[6:8], eng[0:4], eng[4:8]]
    out = {}
    for k, h in enumerate(far):
        out[h] = (codes[k], scales[k], lists[k], k // 4)
    for h in near:
        rest = [e for e in topo.engines(me, T.cores[h]) if e not in eng]
        out[h] = ([rest[0]], [rest[2]], [rest[0], rest[2]], 1)
    return out


def rank_program(g, core, T, topo):
    r = T.rank_of(core)
    if r is None:
        return
    n_ranks = len(T.cores)
    eng = {"v": g.vector, "a": g.scalar, "p": g.tensor, "g": g, "s": g.sync}
    own = {"v": "cv", "a": "ca", "p": "cp", "g": "cg"}
    count = {"cv": 0, "ca": 0, "cp": 0, "cg": 0, "sent": 0}
    waited = {q: {} for q in eng}
    lastw, readers = {}, {}

    def need(q, reads, writes):
        deps = {}
        for k in list(reads) + list(writes):
            if k in lastw:
                s, v = lastw[k]
                deps[s] = max(deps.get(s, 0), v)
        for k in writes:
            for s, v in readers.get(k, []):
                deps[s] = max(deps.get(s, 0), v)
        for s, v in deps.items():
            if q == "p" and s == "cp":
                continue
            if waited[q].get(s, 0) < v:
                eng[q].wait_ge(T.sem[s], v)
                waited[q][s] = v

    def mark(tok, reads, writes):
        for k in reads:
            readers.setdefault(k, []).append(tok)
        for k in writes:
            lastw[k] = tok
            readers[k] = []

    def op(q, call, reads, writes):
        need(q, reads, writes)
        s = own[q]
        count[s] += 1
        call().then_inc(T.sem[s], 1)
        mark((s, count[s]), reads, writes)

    def dma(q, out, in_, sem, reads, writes):
        need(q, reads, writes)
        count[sem] = count.get(sem, 0) + 16
        eng[q].dma_start(out, in_).then_inc(T.sem[sem], 16)
        mark((sem, count[sem]), reads, writes)

    V, A = g.vector, g.scalar

    def ts(out, in0, s1, s2, o0, o1, reads, writes):
        if o1 is None:
            op("v", lambda: V.tensor_scalar(out, in0, s1, None, o0), reads, writes)
        else:
            op("v", lambda: V.tensor_scalar(out, in0, s1, s2, o0, o1), reads, writes)

    def tt(out, in0, in1, o, reads, writes):
        op("v", lambda: V.tensor_tensor(out, in0, in1, o), reads, writes)

    def cp(out, in_, reads, writes):
        op("v", lambda: V.tensor_copy(out, in_), reads, writes)

    def act(out, in_, func, reads, writes, **kw):
        op("a", lambda: A.activation(out, in_, func, **kw), reads, writes)

    def fill(ap, c, writes):
        op("v", lambda: V.memset(ap, c), [], writes)

    def tr(out, in_, reads, writes):
        op("v", lambda: V.transpose(out, in_), reads, writes)

    def scan(out, d0, d1, o0, reads, writes):
        op("v", lambda: V.tensor_tensor_scan(out, d0, d1, 0.0, o0, Op.add), reads, writes)

    def iota(out, pat, base, cm, writes):
        op("g", lambda: g.iota(out, pat, base, cm, allow_small_or_imprecise_dtypes=True), [], writes)

    def quant(name, a, b, in_, reads, key):
        op("v", lambda: V.quantize_mx(T[name + "c"][:, a:b], T[name + "s"][:, a:b], in_), reads, [key + "c", key + "s"])

    def pickc(dst, a, b, src, w, off, rk, ok, wk):
        op("v", lambda: V.tensor_copy(T[dst + "c"][:, a:b].bitcast(dt.uint32),
                                      T[src + "c"][:, 0:w].bitcast(dt.uint32).indirect(off)),
           [k + "c" for k in rk] + [ok], [wk + "c"])

    def picks(dst, a, b, src, w, off, rk, ok, wk):
        act(T[dst + "s"][:, a:b], T[src + "s"][:, 0:w].indirect(off), Act.Copy, [k + "s" for k in rk] + [ok], [wk + "s"])

    def pick(*a):
        pickc(*a)
        picks(*a)

    def bank(i, n, a=0):
        return T.ps[:, 512 * i + a:512 * i + a + n]

    def mm(i, ln, la, rn, ra, rb, start, stop, keys):
        rd = []
        for k in keys:
            rd += [k + "c", k + "s"]
        op("p", lambda: g.tensor.matmul_mx(bank(i, rb - ra), T[ln + "c"][:, la:la + 128], T[ln + "s"][:, la:la + 128],
                                           T[rn + "c"][:, ra:rb], T[rn + "s"][:, ra:rb], start, stop), rd, ["b%d" % i])

    masks = [_masks(T, topo, h) for h in range(n_ranks)]

    def remote(hs, part, sides, sem, key):
        need("g", [key], [])
        trs = []
        for h in hs:
            rid, pid, _ = topo.addr(T.cores[h])
            src, dst = sides(h)
            es = masks[r][h][part]
            count["sent"] += len(es)
            trs.append(RemoteDMATransfer(dst_ids=[DstId(rid=rid, pnc=pid)], dma_engine_mask=sum(1 << e for e in es),
                                         remote_sem=T.sem[sem], src=src, dst=dst))
        g.remote_dma_fused(trs, local_sem=T.sem.sent)
        count[sem] = sum(len(masks[h][r][part]) for h in range(n_ranks) if h != r)
        lastw["sent"] = ("sent", count["sent"])

    def block(h):
        return (r - h) % n_ranks

    def send(t):
        for part, sfx in ((0, "c"), (1, "s")):
            def sides(h):
                a, b = FAR * t + PAIR * h, FAR * t + BLK * block(h)
                src, dst = T["mc0" + sfx][:, a:a + PAIR], T["ld" + sfx][:, b:b + PAIR]
                return (src.bitcast(dt.uint8), dst.bitcast(dt.uint8)) if part == 0 else (src, dst)
            sem = "arr%s%d" % (sfx, t)
            remote(sorted(masks[r]), part, sides, sem, ("m0", "c0")[t] + sfx)
            lastw["land%d%s" % (t, sfx)] = (sem, count[sem])

    def send_lists():
        for call in range(2):
            remote([h for h in sorted(masks[r]) if masks[r][h][3] == call], 2,
                   lambda h: (T.ol[:, 2 * h:2 * h + 2], T.lst[:, 2 * block(h) - 2:2 * block(h)]), "arrl", "ol")
        lastw["lst"] = ("arrl", count["arrl"])

    kbase = 69632.0
    b16 = 2304.0

    for k in range(4):
        dma("s" if k % 2 == 0 else "a", T.wr[32 * k:32 * k + 32, 0:6], T.rev[:], "ldr", [], ["wr%d" % k])
    lastw["wr"] = ("ldr", count["ldr"])
    dma("s", T.mt[:, 0:4 * E], T.m[:], "ldm", [], ["mt0"])
    dma("a", T.mt[:, 4 * E:960], T.b[:], "ldm", [], ["mt"])
    dma("s", T.ut[:], T.u[:], "ldu", [], ["ut"])
    dma("s", T.wt[:], T.w[:], "ldw", [], ["wt"])

    slot = T.sm[:, 0:2]
    iota(T.blf[:], [[1, 6], [0, 2]], 0, 0, ["blf"])
    iota(T.erow[:], [[16, 6], [1, 16], [96, 2]], 0, 0, ["erow"])
    iota(slot, [[64, 2]], 0, 1, ["slot"])
    iota(T.tin[:, 0:32], [[8, 2], [0, 16]], 0, 0, ["tin0"])
    iota(T.src0[:], [[16, 6], [1, 8], [96, 2]], 0, 0, ["src0"])
    iota(T.tin[:, 32:48], [[1, 8], [7, 2]], 0, 0, ["tin1"])
    iota(T.tin[:, 48:64], [[1, 8], [-6, 2]], 6, 0, ["tin2"])
    iota(T.tin[:, 64:96], [[0, 2], [1, 16]], 0, 0, ["tin3"])
    fill(T.wsel[:], 0.0, ["w0", "w1", "w2"])
    cp(T.bl[:], T.blf[:], ["blf"], ["bl"])
    fill(T.swin[:], 0.0, ["swin"])
    fill(T.etp[:], 1.0, ["etp"])
    fill(T.sw[:], 0, ["sw"])
    act(T.xt[:], T.wsel[:], Act.Copy, ["w0", "w1", "w2"], ["xt0", "xt1", "xtc", "xh00", "xh01", "xh10", "xh11"])
    tr(T.econ[:], T.erow[:], ["erow"], ["econ"])
    act(T.qi[:, 0:2], slot, Act.Identity, ["slot"], ["qi"], scale=1.0 / 48, bias=136.0 - 23.5 / 48)
    act(T.qi[:, 2:4], slot, Act.Identity, ["slot"], ["qh"], scale=1.0 / PAIR, bias=136.0 - 11.5 / PAIR)
    act(T.pe[:, 1:5:3], slot, Act.Copy, ["slot"], ["pe1"])
    act(T.sm[:, 2:4], T.qi[:, 0:2], Act.Identity, ["qi"], ["sbase"], scale=48.0, bias=-136.0 * 48)
    act(T.sm[:, 10:12], T.qi[:, 2:4], Act.Identity, ["qh"], ["h8"], scale=float(BLK - PAIR), bias=-136.0 * (BLK - PAIR))
    odd8, pm16 = T.tab[:, 0:1], T.tab[:, 64:65]

    ts(T.hb[:, 0:6], T.wr[:, 0:6], 512.0 / E, kbase - 95.5 * 512.0 / E, Op.mult, Op.add, ["wr"], ["hb"])
    cp(T.revf[:, 0:6], T.wr[:, 0:6], ["wr"], ["revf"])
    tt(T.kb[:], T.hb[:, 0:6].indirect(T.bl[:]), T.econ[:], Op.add, ["hb", "bl", "econ"], ["kb"])
    act(T.revb[:], T.revf[:, 0:6].indirect(T.bl[:]), Act.Copy, ["revf", "bl"], ["revb"])
    tr(T.tab[:, 0:32], T.tin[:, 0:32], ["tin0"], ["tab0"])
    tr(T.krow[:], T.kb[:], ["kb"], ["krow"])
    act(T.src[:], T.src0[:], Act.Identity, ["src0", "tab0"], ["src"], bias=odd8)

    def rank_a(row, col, x, b, j, rk, wk):
        act(T.junk[:, E * j:E * j + E], row, Act.Sign, rk, [wk], bias=col[:, 32 * b:32 * b + 1], scale=-1.0,
            accum_out=x[:, b:b + 1])

    for b in range(4):
        rank_a(T.krow[:], T.kb, T.xk, b, b, ["krow", "kb"], "xk%d" % b)
    for x in range(2):
        ts(T.cmp[:, E * x:E * x + E], T.krow[:], T.kb[:, 128 + 32 * x:129 + 32 * x], None, Op.is_lt, None, ["krow", "kb"],
           ["cmp%d" % x])
    for x in range(2):
        scan(T.csum[:, 96 * x:96 * x + 96], T.cmp[:, E * x:E * x + 96], T.cmp[:, E * x + 96:E * x + E], Op.add,
             ["cmp%d" % x], ["cs%d" % x])
    tr(T.rrow[:], T.revb[:], ["revb"], ["rrow"])
    ts(T.qoff[:, 4:6], T.csum[:, 95:E:96], 16.0, None, Op.add, None, ["cs0", "cs1"], ["qoff1"])
    quant("q0", 0, 240, T.mt[:], ["mt"], "q0")
    xk = ["xk%d" % b for b in range(4)]
    xr = ["xr%d" % b for b in range(6)]
    for b in range(6):
        rank_a(T.rrow[:], T.revb, T.xr, b, 4 + b, ["rrow", "revb"], "xr%d" % b)
    ts(T.qoff[:, 0:4], T.xk[:, 0:4], 0.5, 95.5 + 16.0, Op.mult, Op.add, xk, ["qoff0"])
    tr(T.tab[:, 32:96], T.tin[:, 32:96], ["tin1", "tin2", "tin3"], ["tab"])
    cp(T.swin[:].indirect(T.qoff[:]), T.src[:], ["qoff0", "qoff1", "src"], ["swin"])
    cp(T.slist[:, 0:1], T.tab[:, 32:33], ["tab"], ["slist"])
    tr(T.swt[:, 0:E], T.swin[:, 16:16 + E], ["swin"], ["swt0"])
    tr(T.swt[:, E:416], T.swin[:], ["swin"], ["swt1"])
    ts(T.lt[:, 0:6], T.hb[:, 0:6], 1.0 / 32, 191.0 - kbase / 32 - 2.0 * BLK * r, Op.mult, Op.add, ["hb"], ["lt0"])
    tt(T.sw[:, 0:13], T.swt[:, 0:416:32], T.swt[:, 16:416:32], Op.add, ["swt0", "swt1"], ["sw"])
    ts(T.lt[:, 8:14], T.hb[:, 0:6], kbase + 512.0 * r, 2.0 * FAR, Op.is_lt, Op.mult, ["hb"], ["lt1"])
    cp(T.soff[:], T.sw[:].indirect(T.slist[:, 0:1]), ["sw", "slist"], ["soff"])
    tt(T.lt[:, 16:22], T.lt[:, 0:6], T.lt[:, 8:14], Op.add, ["lt0", "lt1"], ["lt2"])
    pick("mc0", 0, E, "q0", E, T.soff[:, 0:12], ["q0"], "soff", "m0")

    op("g", lambda: g.affine_select(T.etp[:], T.etp[:], [[-1, 528]], Op.is_equal, 0.0, 3, 4), [], ["etp"])
    iota(T.c16[:, 24:40], [[16, 16]], int(b16), 0, ["c16"])
    iota(T.n48[:], [[1, 48]], 0, 0, ["n48"])
    send(0)
    iota(T.c16[:, 0:24], [[0, 2], [16, 12]], int(b16), 0, ["c12"])
    iota(T.i16[:], [[0, 8], [1, 16]], 0, 0, ["i16", "pool"])
    iota(T.wsel[0:1, 2:512:4], [[0, 8], [1, 16]], 0, 0, ["w2a"])
    iota(T.wsel[0:1, 3:512:4], [[0, 128]], 1, 0, ["w2b"])

    def xrow(p, t, a, n, pat, base):
        iota(T.xt[p:p + 1, 4 * a + t:4 * (a + n):4], pat, base, 0, ["xtc"])

    xrow(0, 2, XE, 12, [[0, 12]], 1)
    xrow(0, 3, XE, 12, [[16, 12]], 0)
    xrow(0, 2, XS, 16, [[0, 8], [-1, 2]], 1)
    if r > 0:
        xrow(0, 3, XS, 2 * r, [[-BLK, r], [16, 2]], BLK * r)
    xrow(0, 3, XS + 2 * r, 2, [[16, 2]], 16 * (PAIR * r // 16))
    if r < n_ranks - 1:
        xrow(0, 3, XS + 2 * r + 2, 14 - 2 * r, [[-BLK, n_ranks - 1 - r], [16, 2]], BLK * (n_ranks - 1))
    iota(T.wsel[32:33, 2:512:4], [[0, 16], [1, 8]], 0, 0, ["w2c", "pool"])
    iota(T.wsel[32:33, 3:512:4], [[0, 128]], 1, 0, ["w2"])
    xrow(32, 2, XS, 16, [[0, 8], [1, 2]], 0)
    xrow(32, 3, XS + 2 * r, 2, [[0, 2]], PAIR * r % 16)

    sd = T.sw[:, 0:6]
    tt(T.l32[:, 0:6], T.xr[:, 0:6], T.lt[:, 16:22], Op.add, xr + ["lt2"], ["l32"])
    act(T.lb[:], T.l32[:, 0:6].indirect(T.bl[:]), Act.Copy, ["l32", "bl"], ["lb"], scale=0.5)
    ts(T.fi[:, 8:14], sd, 3, None, Op.bitwise_and, None, ["sw"], ["fj"])
    ts(T.fi[:, 0:6], sd, 252, None, Op.bitwise_and, None, ["sw"], ["fb"])
    ts(T.ff[:, 32:38], sd, 96.0, -95.5, Op.is_ge, Op.mult, ["sw"], ["fg"])
    cp(T.fi[:, 32:48], T.soff[:], ["soff"], ["s32"])
    for k in range(3):
        ts(T.ff[:, 6 * k:6 * k + 6], T.fi[:, 8:14], float(k + 1), float(k), Op.is_lt, Op.add, ["fj"], ["ft%d" % k])
    tt(T.ff[:, 24:30], T.fi[:, 0:6], T.ff[:, 32:38], Op.add, ["fb", "fg"], ["fh"])
    ts(T.fi[:, 48:64], T.fi[:, 32:48], 2, None, Op.arith_shift_right, None, ["s32"], ["s4"])
    ts(T.lt[:, 24:26], T.c16[:, 24:26], pm16, PAIR * r - b16, Op.add, Op.add, ["c16", "tab"], ["lt3"])
    for k in range(3):
        tt(T.ff[:, 40 + 6 * k:46 + 6 * k], T.ff[:, 6 * k:6 * k + 6], T.ff[:, 24:30], Op.add, ["ft%d" % k, "fh"], ["ff%d" % k])
    tr(T.lrow[:], T.lb[:], ["lb"], ["lrow"])
    for x in range(2):
        ts(T.foff[:, x:36:2], T.ff[:, 40:58], 2.0, None, Op.mult, None, ["ff0", "ff1", "ff2"], ["foff%d" % x])
    act(T.ag[:], T.lrow[:].indirect(T.foff[:]), Act.Copy, ["lrow", "foff0", "foff1"], ["ag"])
    ts(T.boff[:], T.fi[:, 48:64], float(E), None, Op.add, None, ["s4"], ["boff"])
    ts(T.ownl[:], T.lt[:, 24:26], E - 1.0, None, Op.min, None, ["lt3"], ["ownl"])
    for b in range(4):
        quant("ep", 128 * b, 128 * b + 128, T.etp[:, 3 - b:515 - b], ["etp"], "ep%d" % b)
    pick("bx", 0, E, "q0", 240, T.boff[:, 0:12], ["q0"], "boff", "bx")
    pick("ld", 0, BLK, "mc0", E, T.ownl[:], ["m0"], "ownl", "own0")
    tr(T.agt[:], T.ag[:], ["ag"], ["agt"])
    act(T.etn[:, 0:516], T.etp[:, 0:516], Act.Copy, ["etp"], ["etn"], scale=-1.0)
    for b in range(4):
        mm(b, "ep", 128 * b, "bx", 0, E, True, False, ["ep%d" % b, "bx"])
    for q in range(2):
        cp(T.pe[32 * q:32 * q + 32, 2:3], T.sw[32 * q:32 * q + 32, q:q + 1], ["sw"], ["pa%d" % q])
    tt(T.pe[:, 0:4:3], slot, T.sm[:, 10:12], Op.add, ["slot", "h8"], ["pe0"])
    cp(T.aoff[:], T.agt[:, 0:3 * E:16], ["agt"], ["aoff"])
    for q in range(2, 4):
        cp(T.pe[32 * q:32 * q + 32, 2:6:3], T.sw[32 * q:32 * q + 32, q:q + 3:2], ["sw"], ["pa%d" % q])
    fill(T.pe[0:64, 3:6], 300.0, ["pe0", "pe1"])
    tt(T.sm[:, 4:6], slot, T.sm[:, 2:4], Op.subtract, ["slot", "sbase"], ["sown"])
    ts(T.sm[:, 6:8], T.sm[:, 2:4], pm16, -b16, Op.add, Op.add, ["sbase", "tab"], ["sbp"])
    pes = ["pe0", "pe1"] + ["pa%d" % q for q in range(4)]
    act(T.hi[:, 0:6], T.pe[:, 0:6], Act.Identity, pes, ["hi"], bias=b16 - 7.5)
    ts(T.sm[:, 16:64], T.n48[:], float(PAIR), None, Op.is_ge, None, ["n48"], ["ge24"])
    fill(T.zoff[:], 0, ["zoff"])
    fill(T.rst[:], 1.0, ["rst"])
    ts(T.sm[:, 8:10], T.sm[:, 4:6], float(PAIR), None, Op.is_ge, None, ["sown"], ["sfl"])
    for x in range(2):
        ts(T.cl[:, 4 * x:4 * x + 3], T.c16[:, 24:27], T.sm[:, 6 + x:7 + x], None, Op.add, None, ["c16", "sbp"], ["cl%d" % x])
    tt(T.pe[:, 8:14], T.pe[:, 0:6], T.hi[:, 0:6], Op.subtract, pes + ["hi"], ["pd"])
    act(T.hi[:, 8:10], T.hi[:, 1:5:3], Act.Identity, ["hi"], ["hv"], bias=-b16)
    act(T.hi[:, 10:12], T.pe[:, 9:13:3], Act.Identity, ["pd"], ["lv"], bias=b16)
    for x in range(2):
        for k, (a, n, c) in ((0, (24, 16, 24)), (2, (0, 24, 0))):
            ts(T.k8[:, 40 * x + a:40 * x + a + n], T.c16[:, c:c + n], T.hi[:, 3 * x + k:3 * x + k + 1], float(CAP),
               Op.is_equal, Op.mult, ["c16", "c12", "hi"], ["k8%d%d" % (x, k)])

    def wrow(k, x):
        j = 8 + 2 * k + 3 * x
        ts(T.wsel[:, x:512:4], T.i16[:], -b16, T.pe[:, j:j + 1], Op.add, Op.is_equal, ["i16", "pd"], ["w%d" % x])

    def wquant(k):
        quant("wq", 128 * k, 128 * k + 128, T.wsel[:, 0:512], ["w0", "w1", "w2"], "wq%d" % k)

    def digits(x, k):
        a = (XH, XL)[k]
        ts(T.xt[:, 4 * a + x:4 * a + 48:4], T.c16[:, 0:12], T.hi[:, 3 * x + 2:3 * x + 3],
           T.hi[:, 8 + 2 * k + x:9 + 2 * k + x], Op.is_equal, Op.mult, ["c12", "hi", "hv", "lv"], ["xh%d%d" % (x, k)])

    def side(t, step):
        if (t, step) == (0, 0):
            wrow(0, 0)
            wrow(0, 1)
            for b in range(4):
                quant("en", 128 * b, 128 * b + 128, T.etn[:, 3 - b:515 - b], ["etn"], "en%d" % b)
            quant("qu", 0, 128, T.ut[:], ["ut"], "qu")
            wquant(0)
        elif (t, step) == (0, 1):
            for x in range(2):
                ts(T.t1[:, 48 * x:48 * x + 48], T.n48[:], T.sm[:, 4 + x:5 + x], -1e-33, Op.is_lt, Op.mult, ["n48", "sown"],
                   ["t1%d" % x])
                ts(T.t2[:, 48 * x:48 * x + 48], T.sm[:, 16:64], T.sm[:, 8 + x:9 + x], 1e29, Op.not_equal, Op.mult,
                   ["ge24", "sfl"], ["t2%d" % x])
            pick("ur", 0, 128, "qu", 128, T.zoff[:], ["qu"], "zoff", "ur")
        elif (t, step) == (0, 2):
            fill(T.rst[:, 0:96:48], 0.0, ["rst"])
        elif (t, step) == (0, 3):
            tt(T.thr[:], T.t1[:], T.t2[:], Op.add, ["t10", "t11", "t20", "t21"], ["thr"])
            digits(0, 0)
            digits(0, 1)
        elif (t, step) == (0, 4):
            digits(1, 0)
        elif t == 0 and step in (5, 6):
            wrow(1, step - 5)
        elif (t, step) == (0, 7):
            digits(1, 1)
        elif (t, step) == (0, 8):
            wquant(1)
        elif (t, step) == (1, 0):
            cp(T.ya[:, 0:E], bank(4, E), [], ["b4", "ya0"])
            act(T.yb[:, 0:E], bank(5, E), Act.Copy, [], ["b5", "yb0"])
            dma("s", T.y[:, 0:E], T.ya[:, 0:E], "sty", ["ya0", "sent"], [])
            dma("s", T.y[:, E:2 * E], T.yb[:, 0:E], "sty", ["yb0", "sent"], [])
            pickc("m1", 0, E, "me", E, T.soff[:, 0:12], ["m1e"], "soff", "m1")
            cp(T.m1s[:], T.mes[:, 0:E].indirect(T.soff[:, 0:12]), ["m1es", "soff"], ["m1s"])
        elif (t, step) == (1, 1):
            pickc("me", FAR, FAR + E, "c1", E, T.poff[:], ["c1"], "poff", "ce")
        elif (t, step) == (1, 3):
            picks("me", FAR, FAR + E, "c1", E, T.poff[:], ["c1"], "poff", "ce")

    def one_round(t):
        land, an = ("ld", "nl")[t], "a%d" % t
        held, (cand, c0) = ("mc0", "m1")[t], (("mc0", FAR), ("c1", 0))[t]
        for k in range(3):
            pick(an, E * k, E * k + E, land, FAR, T.aoff[:, 12 * k:12 * k + 12],
                 [("land0", "nl")[t], "own%d" % t], "aoff", "%s%d" % (an, k))
        side(t, 0)
        for k, b in ((0, 0), (0, 1), (0, 2), (0, 3), (1, 0), (1, 1), (2, 0), (2, 1), (1, 2), (2, 2), (1, 3), (2, 3)):
            mm(b, "ep", 128 * b, an, E * k, E * k + E, False, k == 2, ["ep%d" % b, "%s%d" % (an, k)])
        for b in range(4):
            mm(4 + b, "en", 128 * b, held, 0, E, True, False, ["en%d" % b, "m%d" % t])
        for b in range(3):
            act(T.zt[:, b:4 * E:4], bank(b, E), Act.Copy, [], ["b%d" % b, "z%d" % b], scale=0.25)
        ts(T.zt[:, 3:4 * E:4], bank(3, E), 0.25, None, Op.mult, None, [], ["b3", "z3"])
        quant(cand, c0, c0 + E, T.zt[:], ["z0", "z1", "z2", "z3"], "c%d" % t)
        if t == 0:
            send(1)
        side(t, 1)
        for b in range(4):
            mm(4 + b, "ep", 128 * b, cand, c0, c0 + E, False, True, ["ep%d" % b, "c%d" % t])
        for b in range(4):
            if b % 2 == 0:
                act(T.yt[:, b:4 * E:4], bank(4 + b, E), Act.Copy, [], ["b%d" % (4 + b), "y%d" % b])
            else:
                cp(T.yt[:, b:4 * E:4], bank(4 + b, E), [], ["b%d" % (4 + b), "y%d" % b])
        side(t, 2)
        quant("yq", 0, E, T.yt[:], ["y0", "y1", "y2", "y3"], "yq")
        side(t, 3)
        mm(0, "ur", 0, "yq", 0, E, True, True, ["ur", "yq"])
        mm(1, "yq", 0, "ur", 0, 128, True, True, ["ur", "yq"])
        mm(2, "yq", 64, "ur", 0, 128, True, True, ["ur", "yq"])
        if t == 1:
            for o in range(2):
                mm(4 + o, "qw", 128 * o, "me", FAR, FAR + E, True, True, ["qw%d" % o, "ce"])
            mm(6, "xq", 0, "wq", 128, 256, True, False, ["xq0", "wq1"])
        act(T.arow[:], bank(0, E), Act.Abs, [], ["b0", "arow"])
        for x in range(2):
            op("v", lambda: V.tensor_reduce(T.ncol[:, x:x + 1], bank(1 + x, 1), AxisListType.X, Op.max, negate=True,
                                            apply_absolute_value=True), [], ["b%d" % (1 + x), "ncol%d" % x])
        side(t, 4)
        act(T.dd[:, 0:48], T.arow[:].indirect(T.cl[:, 0:3]), Act.Identity, ["arow", "cl0", "ncol0"], ["dd0"],
            bias=T.ncol[:, 0:1])
        ts(T.dd[:, 48:96], T.arow[:].indirect(T.cl[:, 4:7]), T.ncol[:, 1:2], None, Op.add, None, ["arow", "cl1", "ncol1"], ["dd1"])
        if t == 1:
            act(T.ya[:, FAR:FAR + E], bank(4, E), Act.Copy, [], ["b4", "yac"])
            act(T.yb[:, FAR:FAR + E], bank(5, E), Act.Copy, [], ["b5", "ybc"])
        side(t, 5)
        tt(T.beats[:], T.dd[:], T.thr[:], Op.is_gt, ["dd0", "dd1", "thr"], ["beats"])
        side(t, 6)
        scan(T.cnt[:], T.rst[:], T.beats[:], Op.mult, ["beats", "rst"], ["cnt"])
        side(t, 7)
        n = (40, 24)[t]
        for x in range(2):
            ts(T.xt[:, 4 * XU + x:4 * (XU + n):4], T.k8[:, 40 * x:40 * x + n], T.cnt[:, 48 * x + 47:48 * x + 48], float(FAR),
               Op.is_gt, Op.mult, ["k8%d0" % x, "k8%d2" % x, "cnt"], ["xt%d" % x])
        w = (XW, 128)[t]
        quant("xq", X1 * t, X1 * t + w, T.xt[:, 0:4 * w], ["xt0", "xt1", "xtc", "xh00", "xh01", "xh10", "xh11"], "xq%d" % t)
        side(t, 8)
        mm(3, "wq", 128 * t, "xq", X1 * t, X1 * t + 128, True, True, ["wq%d" % t, "xq%d" % t])

    one_round(0)
    cp(T.ol[:], bank(3, 16, XS), [], ["b3", "ol"])
    send_lists()

    for k in range(3):
        mm(6, "wq", 128, "xq", 12 * k, 12 * k + 128, k == 0, k == 2, ["wq1", "xq0"])
    for k in range(2):
        mm(5, "wq", 128, "xq", 12 * k, 12 * k + 128, k == 0, k == 1, ["wq1", "xq0"])
    fill(T.ya[:, E:FAR], 0.0, ["yag"])
    fill(T.yb[:, E:FAR], 0.0, ["ybg"])
    pick("nl", 0, BLK, "mc0", FAR + E, T.ol[:, 2 * r:2 * r + 2], ["m0", "c0"], "ol", "own1")
    for b in range(4):
        mm(b, "ep", 128 * b, "bx", 0, E, True, False, ["ep%d" % b, "bx"])
    cp(T.moff[:], bank(6, 12), [], ["b6", "moff"])
    for o in range(2):
        quant("qw", 128 * o, 128 * o + 128, T.wt[:, 512 * o:512 * o + 512], ["wt"], "qw%d" % o)
    pick("me", 0, E, "mc0", FAR + E, T.moff[:], ["m0", "c0"], "moff", "m1e")
    cp(T.poff[:], bank(5, 12), [], ["b5", "poff"])
    for o in range(2):
        mm(4 + o, "qw", 128 * o, "me", 0, E, True, True, ["qw%d" % o, "m1e"])

    pick("nl", BLK, FAR, "ld", 2 * FAR, T.lst[:, 0:14], ["land0", "land1", "own0"], "lst", "nl")
    one_round(1)
    cp(T.offe[:], bank(3, 12, XE), [], ["b3", "offe"])
    mm(6, "xq", X1, "wq", 128, 256, False, True, ["xq1", "wq1"])
    cp(T.yo[:, 0:E], T.ya[:].indirect(T.offe[:]), ["ya0", "yag", "yac", "offe"], ["yo0"])
    act(T.yo[:, E:2 * E], T.yb[:].indirect(T.offe[:]), Act.Copy, ["yb0", "ybg", "ybc", "offe"], ["yo1"])
    pick("mo", 0, E, "me", FAR + E, T.offe[:], ["m1e", "ce"], "offe", "mo")
    ts(T.upo[0:64, :], T.ps[0:64, 3072:3088], 1.0 / FAR, None, Op.mult, None, [], ["b6", "upo"])
    dma("s", T.y[:, 2 * E:3 * E], T.yo[:, 0:E], "sto", ["yo0"], [])
    dma("s", T.y[:, 3 * E:4 * E], T.yo[:, E:2 * E], "sto", ["yo1"], [])
    dma("s", T.oc[:], T.moc[:].bitcast(dt.uint8), "sto", ["moc"], [])
    for k in range(4):
        dma("s" if k == 0 else "a", T.osc[4 * k:4 * k + 4, :], T.mos[32 * k:32 * k + 4, :], "sto", ["mos"], [])
    dma("s", T.up[:], T.upo[XU:XU + 12, :], "sto", ["upo"], [])

    for s in SEMAPHORES:
        if count.get(s, 0) > 0:
            g.wait_ge(T.sem[s], count[s])
